import numpy as np
import ml_dtypes


def mxq(x, axis, fmt="e4m3"):
    dtype, down = {"e4m3": (ml_dtypes.float8_e4m3fn, 7), "e5m2": (ml_dtypes.float8_e5m2, 14)}[fmt]
    v = np.moveaxis(np.asarray(x, np.float32).astype(ml_dtypes.bfloat16).astype(np.float64), axis, -1)
    blocks = v.reshape(v.shape[:-1] + (-1, 32))
    amax = np.abs(blocks).max(-1, keepdims=True)
    byte = np.maximum(np.where(amax > 0, np.frexp(amax)[1] - 1 + 127, 0) - down, 1)
    scale = np.exp2(byte - 127.0)
    codes = (blocks / scale).astype(np.float32).astype(dtype).astype(np.float64)
    return np.moveaxis((codes * scale).reshape(v.shape), -1, axis)


WIDE = False


def mx_kscale(k):
    if not WIDE:
        return np.ones(k)
    levels = np.array([10, -10, 5, -5, 0])
    if k % 512:
        return np.exp2(np.random.permutation(np.resize(levels, k // 32))).repeat(32)
    a = np.empty((k // 512, 16))
    for p in range(k // 512):
        a[p, :8] = np.random.permutation(np.resize(levels, 8))
        for g in range(8):
            far = levels[np.abs(levels - a[p, g]) >= 10]
            a[p, g + 8] = far[np.random.randint(len(far))]
    return np.exp2(a.ravel()).repeat(32)


def f64(x):
    return np.asarray(x).astype(np.float64)


def striped(idx):
    return np.tile(idx.reshape(-1, 16).T, (8, 1)).astype(np.uint16)


def unstriped(offs):
    return offs[:16].T.reshape(-1).astype(np.int64)


def pack_weight(w):
    k, n = w.shape
    w = f64(np.asarray(w, np.float32).astype(ml_dtypes.bfloat16)).reshape(k // 32, 32, n)
    amax = np.abs(w).max(1)
    byte = np.clip(np.where(amax > 0, np.frexp(amax)[1] - 1 + 127 - 7, 1), 1, 254)
    scaled = (w * np.exp2(127.0 - byte)[:, None, :]).reshape(k, n).astype(np.float32)
    words = np.ascontiguousarray(scaled.reshape(k // 512, 128, 4, n).transpose(0, 1, 3, 2)).astype(ml_dtypes.float8_e4m3fn).view(np.uint8)
    return words, np.ascontiguousarray(byte.astype(np.uint8).reshape(k // 512, 16, n))


def unpack_weight(words, scales):
    g, p, n, _ = words.shape
    vals = np.ascontiguousarray(words).view(ml_dtypes.float8_e4m3fn).astype(np.float64) * np.repeat(np.exp2(scales.astype(np.float64) - 127.0), 8, axis=1)[..., None]
    return vals.transpose(0, 1, 3, 2).reshape(g * 512, n)


def gelu(v):
    return 0.5 * v * (1.0 + np.tanh(np.sqrt(2.0 / np.pi) * (v + 0.044715 * v**3)))


K, T, S, H, N = 512, 2048, 1024, 512, 256


def setup_inputs():
    n = np.random.standard_normal
    s = mx_kscale(K)[:, None]
    u = mx_kscale(H)
    packed_xT = pack_weight(n((K, T)) * s)
    packed_w1 = pack_weight(n((K, N)) / np.sqrt(2 * K) / s)
    packed_w3 = pack_weight(n((H, N)) / np.sqrt(2 * H) / u[:, None])
    return {
        "x_words": packed_xT[0],
        "x_scales": packed_xT[1],
        "w1_words": packed_w1[0],
        "w1_scales": packed_w1[1],
        "w2": (n((K, H)) / np.sqrt(K) / s * u).astype(np.float32),
        "w3_words": packed_w3[0],
        "w3_scales": packed_w3[1],
        "offs": striped(np.random.permutation(T)[:S]),
    }


def reference(x_words, x_scales, w1_words, w1_scales, w2, w3_words, w3_scales, offs):
    xq = unpack_weight(x_words, x_scales)[:, unstriped(offs)]
    h = gelu(mxq(f64(w2), 0, "e4m3").T @ xq)
    return unpack_weight(w1_words, w1_scales).T @ xq + unpack_weight(w3_words, w3_scales).T @ mxq(h, 0, "e4m3")

@@ -1,0 +1,139 @@
+from contextlib import ExitStack
+
+import concourse.mybir as mybir
+
+K, T, S, H, N = 512, 2048, 1024, 512, 256
+FLOPS = 2 * S * (K * H + K * N + H * N)
+
+F32 = mybir.dt.float32
+BF16 = mybir.dt.bfloat16
+I32 = mybir.dt.int32
+U32 = mybir.dt.uint32
+U16 = mybir.dt.uint16
+U8 = mybir.dt.uint8
+FP8X4 = mybir.dt.float8_e4m3fn_x4
+GELU = mybir.ActivationFunctionType.Gelu_apprx_tanh
+
+P = 128
+PACK = 4
+GATHER = 256
+SUB = 128
+CHUNKS = [256, 256, 256, 128, 128]
+
+
+def load_scales(queue, plane, scales):
+    for q in range(4):
+        queue.dma_start(out=plane[32 * q : 32 * q + 4, :].bitcast(I32), in_=scales[0, 4 * q : 4 * q + 4, :].bitcast(I32))
+
+
+def words_of(dram):
+    return dram[0].rearrange("p n t -> p (n t)").bitcast(I32)
+
+
+def tile_picked_lora_gelu_p_kernel(tc, x_words, x_scales, w1_words, w1_scales, w2, w3_words, w3_scales, offs, out):
+    nc = tc.nc
+    with ExitStack() as ctx:
+        keep = ctx.enter_context(tc.tile_pool(name="keep", bufs=1))
+        hps = ctx.enter_context(tc.psum_pool(name="hps", bufs=4))
+        ops = ctx.enter_context(tc.psum_pool(name="ops", bufs=2))
+        lps = ctx.enter_context(tc.psum_pool(name="lps", bufs=1))
+
+        offsets = keep.tile([P, S // 16], U16, name="offsets")
+        xs = keep.tile([P, T], U8, name="xs", align_bytes=64)
+        xw = keep.tile([P, T], U32, name="xw", align_bytes=64)
+        ws = keep.tile([P, 2 * N], U8, name="ws", align_bytes=64)
+        ww = keep.tile([P, 2 * N], U32, name="ww", align_bytes=64)
+        raw = [keep.tile([P, PACK, H // 2], F32, name=f"raw{a}", align_bytes=64) for a in range(2)]
+        w2b = keep.tile([P, PACK, P, PACK], BF16, name="w2b", align_bytes=64)
+        w2w = keep.tile([P, H], U32, name="w2w", align_bytes=64)
+        w2s = keep.tile([P, H], U8, name="w2s", align_bytes=64)
+        gs = keep.tile([P, S], U8, name="gs", align_bytes=64)
+        gw = [keep.tile([P, GATHER], U32, name=f"gw{g}", align_bytes=64) for g in range(S // GATHER)]
+        warm = keep.tile([P, 2], F32, name="warm")
+
+        nc.vector.memset(xs[:].bitcast(I32), 0)
+        nc.vector.memset(warm[:, 0:1], 0.0)
+        nc.vector.memset(ws[:].bitcast(I32), 0)
+
+        nc.sync.dma_start(offsets[:], offs)
+        load_scales(nc.scalar, xs, x_scales)
+        nc.scalar.activation(out=warm[:, 1:2], in_=warm[:, 0:1], func=GELU)
+        w2v = w2.rearrange("(p j) c -> p j c", j=PACK)
+        for a in range(2):
+            nc.sync.dma_start(out=raw[a][:], in_=w2v[:, :, a * (H // 2) : (a + 1) * (H // 2)])
+        nc.sync.dma_start(out=xw[:].bitcast(I32), in_=words_of(x_words))
+        nc.sync.dma_start(out=ww[:, 0:N].bitcast(I32), in_=words_of(w1_words))
+        nc.sync.dma_start(out=ww[:, N : 2 * N].bitcast(I32), in_=words_of(w3_words))
+        load_scales(nc.sync, ws[:, 0:N], w1_scales)
+        load_scales(nc.sync, ws[:, N : 2 * N], w3_scales)
+
+        nc.vector.tensor_copy(gs[:], xs[:].indirect(offsets[:]))
+        for a in range(2):
+            nc.scalar.copy(
+                out=w2b[:, :, 64 * a : 64 * (a + 1), :].rearrange("p t m j -> p m j t"),
+                in_=raw[a][:].rearrange("p j (m t) -> p m j t", t=PACK),
+            )
+        for t in range(PACK):
+            cols = slice(t * P, (t + 1) * P)
+            nc.vector.quantize_mx(out=w2w[:, cols].bitcast(FP8X4), scales=w2s[:, cols], in_=w2b[:, t].rearrange("p m j -> p (m j)"))
+        for g in range(S // GATHER):
+            nc.vector.tensor_copy(gw[g][:], xw[:].indirect(offsets[:, g * GATHER // 16 : (g + 1) * GATHER // 16]))
+
+        def x_operand(n0, width):
+            g, o = divmod(n0, GATHER)
+            return gw[g][:, o : o + width].bitcast(FP8X4), gs[:, n0 : n0 + width]
+
+        outv = out.rearrange("(m p) n -> p m n", p=P)
+
+        def hidden(c, n0, width):
+            hb = keep.tile([P, width, PACK], BF16, name=f"hb{c}", align_bytes=64)
+            for s0 in range(0, width, SUB):
+                hp = hps.tile([P, PACK, SUB], F32, name="hp")
+                xq, xsc = x_operand(n0 + s0, SUB)
+                for t in range(PACK):
+                    cols = slice(t * P, (t + 1) * P)
+                    nc.tensor.matmul_mx(out=hp[:, t, :], lhsT=w2w[:, cols].bitcast(FP8X4), lhsT_scale=w2s[:, cols], rhs=xq, rhs_scale=xsc, start=True, stop=True)
+                nc.scalar.activation(out=hb[:, s0 : s0 + SUB, :], in_=hp[:].rearrange("p t n -> p n t"), func=GELU)
+            return hb
+
+        def finish(c, n0, width, hb):
+            last = c == len(CHUNKS) - 1
+            hw = keep.tile([P, width], U32, name=f"hw{c}", align_bytes=64)
+            hs = keep.tile([P, width], U8, name=f"hs{c}", align_bytes=64)
+            xq, xsc = x_operand(n0, width)
+
+            def term(dst, m, second):
+                cols = slice(second * N + m * P, second * N + (m + 1) * P)
+                rhs, rsc = (hw[:].bitcast(FP8X4), hs[:]) if second else (xq, xsc)
+                nc.tensor.matmul_mx(out=dst, lhsT=ww[:, cols].bitcast(FP8X4), lhsT_scale=ws[:, cols], rhs=rhs, rhs_scale=rsc, start=not second, stop=bool(second))
+
+            if last:
+                accs = [lps.tile([P, width], F32, name=f"last{m}") for m in range(2)]
+                for m in range(2):
+                    term(accs[m][:], m, 0)
+            nc.vector.quantize_mx(out=hw[:].bitcast(FP8X4), scales=hs[:], in_=hb[:].rearrange("p n t -> p (n t)"))
+            if last:
+                for m in range(2):
+                    term(accs[m][:], m, 1)
+                res = [keep.tile([P, width], F32, name=f"resl{m}") for m in range(2)]
+                nc.scalar.copy(out=res[0][:], in_=accs[0][:])
+                nc.vector.tensor_copy(out=res[1][:], in_=accs[1][:])
+                nc.scalar.dma_start(out=out[0:P, n0 : n0 + width], in_=res[0][:])
+                nc.sync.dma_start(out=out[P : 2 * P, n0 : n0 + width], in_=res[1][:])
+            else:
+                acc = ops.tile([P, 2, width], F32, name="acc")
+                for m in range(2):
+                    term(acc[:, m, :], m, 0)
+                    term(acc[:, m, :], m, 1)
+                res = keep.tile([P, 2, width], F32, name=f"res{c}")
+                nc.vector.tensor_copy(out=res[:], in_=acc[:])
+                nc.sync.dma_start(out=outv[:, :, n0 : n0 + width], in_=res[:])
+
+        starts = [sum(CHUNKS[:c]) for c in range(len(CHUNKS))]
+        pending = None
+        for c, width in enumerate(CHUNKS):
+            hb = hidden(c, starts[c], width)
+            if pending is not None:
+                finish(*pending)
+            pending = (c, starts[c], width, hb)
+        finish(*pending)

@@ -18,7 +18,9 @@ P = 128
 PACK = 4
 GATHER = 256
 SUB = 128
-CHUNKS = [256, 256, 256, 128, 128]
+CHUNKS = [128] * 8
+EARLY = 768
+SPLIT = 48
 
 
 def load_scales(queue, plane, scales):
@@ -34,61 +36,77 @@ def tile_picked_lora_gelu_p_kernel(tc, x_words, x_scales, w1_words, w1_scales, w
     nc = tc.nc
     with ExitStack() as ctx:
         keep = ctx.enter_context(tc.tile_pool(name="keep", bufs=1))
-        hps = ctx.enter_context(tc.psum_pool(name="hps", bufs=4))
-        ops = ctx.enter_context(tc.psum_pool(name="ops", bufs=2))
-        lps = ctx.enter_context(tc.psum_pool(name="lps", bufs=1))
+        psum = ctx.enter_context(tc.psum_pool(name="psum", bufs=1))
 
         offsets = keep.tile([P, S // 16], U16, name="offsets")
         xs = keep.tile([P, T], U8, name="xs", align_bytes=64)
         xw = keep.tile([P, T], U32, name="xw", align_bytes=64)
-        ws = keep.tile([P, 2 * N], U8, name="ws", align_bytes=64)
-        ww = keep.tile([P, 2 * N], U32, name="ww", align_bytes=64)
-        raw = [keep.tile([P, PACK, H // 2], F32, name=f"raw{a}", align_bytes=64) for a in range(2)]
-        w2b = keep.tile([P, PACK, P, PACK], BF16, name="w2b", align_bytes=64)
+        raw = [keep.tile([P, PACK, H // 2], F32, name=f"raw{a}", tag=f"raw{a}", align_bytes=64) for a in range(2)]
+        w2b = keep.tile([P, PACK, P, PACK], BF16, name="w2b", tag="staged", align_bytes=64)
         w2w = keep.tile([P, H], U32, name="w2w", align_bytes=64)
         w2s = keep.tile([P, H], U8, name="w2s", align_bytes=64)
-        gs = keep.tile([P, S], U8, name="gs", align_bytes=64)
+        warm = keep.tile([P, 2], F32, name="warm", align_bytes=64)
+        ws = keep.tile([P, 2 * N], U8, name="ws", align_bytes=64)
         gw = [keep.tile([P, GATHER], U32, name=f"gw{g}", align_bytes=64) for g in range(S // GATHER)]
-        warm = keep.tile([P, 2], F32, name="warm")
 
         nc.vector.memset(xs[:].bitcast(I32), 0)
         nc.vector.memset(warm[:, 0:1], 0.0)
-        nc.vector.memset(ws[:].bitcast(I32), 0)
-
-        nc.sync.dma_start(offsets[:], offs)
-        load_scales(nc.scalar, xs, x_scales)
+        nc.gpsimd.memset(ws[:].bitcast(I32), 0)
         nc.scalar.activation(out=warm[:, 1:2], in_=warm[:, 0:1], func=GELU)
+
         w2v = w2.rearrange("(p j) c -> p j c", j=PACK)
-        for a in range(2):
-            nc.sync.dma_start(out=raw[a][:], in_=w2v[:, :, a * (H // 2) : (a + 1) * (H // 2)])
+        nc.sync.dma_start(offsets[:], offs)
+        nc.sync.dma_start(out=raw[0][:], in_=w2v[:, :, 0 : H // 2])
+        load_scales(nc.sync, xs, x_scales)
+        nc.sync.dma_start(out=raw[1][:], in_=w2v[:, :, H // 2 : H])
         nc.sync.dma_start(out=xw[:].bitcast(I32), in_=words_of(x_words))
-        nc.sync.dma_start(out=ww[:, 0:N].bitcast(I32), in_=words_of(w1_words))
-        nc.sync.dma_start(out=ww[:, N : 2 * N].bitcast(I32), in_=words_of(w3_words))
-        load_scales(nc.sync, ws[:, 0:N], w1_scales)
+        load_scales(nc.gpsimd, ws[:, 0:N], w1_scales)
         load_scales(nc.sync, ws[:, N : 2 * N], w3_scales)
 
-        nc.vector.tensor_copy(gs[:], xs[:].indirect(offsets[:]))
-        for a in range(2):
-            nc.scalar.copy(
-                out=w2b[:, :, 64 * a : 64 * (a + 1), :].rearrange("p t m j -> p m j t"),
-                in_=raw[a][:].rearrange("p j (m t) -> p m j t", t=PACK),
+        gs = {}
+
+        def gather_scales(n0, n1, tag):
+            tile = keep.tile([P, n1 - n0], U8, name=f"gs{n0}", tag=tag, align_bytes=64)
+            nc.vector.tensor_copy(tile[:], xs[:].indirect(offsets[:, n0 // 16 : n1 // 16]))
+            for n in range(n0, n1, SUB):
+                gs[n] = (tile, n0)
+
+        gather_scales(0, EARLY, "gs_early")
+
+        def regroup(copy, a, m0, m1):
+            copy(
+                out=w2b[:, :, 64 * a + m0 : 64 * a + m1, :].rearrange("p t m j -> p m j t"),
+                in_=raw[a][:, :, PACK * m0 : PACK * m1].rearrange("p j (m t) -> p m j t", t=PACK),
             )
+
+        regroup(nc.scalar.copy, 0, 0, 64)
+        regroup(nc.scalar.copy, 1, 0, SPLIT)
+        regroup(nc.vector.tensor_copy, 1, SPLIT, 64)
+        ww = keep.tile([P, 2 * N], U32, name="ww", tag="raw1", align_bytes=64)
+        nc.scalar.dma_start(out=ww[:, 0:N].bitcast(I32), in_=words_of(w1_words))
+        nc.scalar.dma_start(out=ww[:, N : 2 * N].bitcast(I32), in_=words_of(w3_words))
         for t in range(PACK):
             cols = slice(t * P, (t + 1) * P)
             nc.vector.quantize_mx(out=w2w[:, cols].bitcast(FP8X4), scales=w2s[:, cols], in_=w2b[:, t].rearrange("p m j -> p (m j)"))
+        gather_scales(EARLY, S, "staged")
+        scrap = psum.tile([P, P], F32, name="scrap", tag="bank7")
+        for r in range(12):
+            nc.tensor.matmul_mx(out=scrap[:], lhsT=w2w[:, 0:P].bitcast(FP8X4), lhsT_scale=w2s[:, 0:P], rhs=w2w[:, 0:P].bitcast(FP8X4), rhs_scale=w2s[:, 0:P], start=True, stop=True)
         for g in range(S // GATHER):
-            nc.vector.tensor_copy(gw[g][:], xw[:].indirect(offsets[:, g * GATHER // 16 : (g + 1) * GATHER // 16]))
+            cols = slice(g * GATHER // 16, (g + 1) * GATHER // 16)
+            nc.vector.tensor_copy(gw[g][:], xw[:].indirect(offsets[:, cols]))
 
         def x_operand(n0, width):
             g, o = divmod(n0, GATHER)
-            return gw[g][:, o : o + width].bitcast(FP8X4), gs[:, n0 : n0 + width]
+            tile, first = gs[n0]
+            return gw[g][:, o : o + width].bitcast(FP8X4), tile[:, n0 - first : n0 - first + width]
 
         outv = out.rearrange("(m p) n -> p m n", p=P)
 
         def hidden(c, n0, width):
-            hb = keep.tile([P, width, PACK], BF16, name=f"hb{c}", align_bytes=64)
+            hb = keep.tile([P, width, PACK], BF16, name=f"hb{c}", tag=f"hb{c}", align_bytes=64)
             for s0 in range(0, width, SUB):
-                hp = hps.tile([P, PACK, SUB], F32, name="hp")
+                hp = psum.tile([P, PACK, SUB], F32, name="hp", tag=f"bank{(n0 + s0) // SUB % 4}")
                 xq, xsc = x_operand(n0 + s0, SUB)
                 for t in range(PACK):
                     cols = slice(t * P, (t + 1) * P)
@@ -108,7 +126,7 @@ def tile_picked_lora_gelu_p_kernel(tc, x_words, x_scales, w1_words, w1_scales, w
                 nc.tensor.matmul_mx(out=dst, lhsT=ww[:, cols].bitcast(FP8X4), lhsT_scale=ws[:, cols], rhs=rhs, rhs_scale=rsc, start=not second, stop=bool(second))
 
             if last:
-                accs = [lps.tile([P, width], F32, name=f"last{m}") for m in range(2)]
+                accs = [psum.tile([P, width], F32, name=f"last{m}", tag=f"bank{(c + m + 4) % 8}") for m in range(2)]
                 for m in range(2):
                     term(accs[m][:], m, 0)
             nc.vector.quantize_mx(out=hw[:].bitcast(FP8X4), scales=hs[:], in_=hb[:].rearrange("p n t -> p (n t)"))
@@ -121,12 +139,15 @@ def tile_picked_lora_gelu_p_kernel(tc, x_words, x_scales, w1_words, w1_scales, w
                 nc.scalar.dma_start(out=out[0:P, n0 : n0 + width], in_=res[0][:])
                 nc.sync.dma_start(out=out[P : 2 * P, n0 : n0 + width], in_=res[1][:])
             else:
-                acc = ops.tile([P, 2, width], F32, name="acc")
+                acc = psum.tile([P, 2, width], F32, name="acc", tag=f"bank{(c + 4) % 8}")
                 for m in range(2):
                     term(acc[:, m, :], m, 0)
                     term(acc[:, m, :], m, 1)
                 res = keep.tile([P, 2, width], F32, name=f"res{c}")
-                nc.vector.tensor_copy(out=res[:], in_=acc[:])
+                if c >= len(CHUNKS) - 3:
+                    nc.scalar.copy(out=res[:], in_=acc[:])
+                else:
+                    nc.vector.tensor_copy(out=res[:], in_=acc[:])
                 nc.sync.dma_start(out=outv[:, :, n0 : n0 + width], in_=res[:])
 
         starts = [sum(CHUNKS[:c]) for c in range(len(CHUNKS))]

@@ -19,12 +19,12 @@ PACK = 4
 GATHER = 256
 SUB = 128
 CHUNKS = [128] * 8
-EARLY = 768
-SPLIT = 48
+EARLY = 1024
+SPLIT = 64
 
 
-def load_scales(queue, plane, scales):
-    for q in range(4):
+def load_scales(queue, plane, scales, quadrants=range(4)):
+    for q in quadrants:
         queue.dma_start(out=plane[32 * q : 32 * q + 4, :].bitcast(I32), in_=scales[0, 4 * q : 4 * q + 4, :].bitcast(I32))
 
 
@@ -45,23 +45,21 @@ def tile_picked_lora_gelu_p_kernel(tc, x_words, x_scales, w1_words, w1_scales, w
         w2b = keep.tile([P, PACK, P, PACK], BF16, name="w2b", tag="staged", align_bytes=64)
         w2w = keep.tile([P, H], U32, name="w2w", align_bytes=64)
         w2s = keep.tile([P, H], U8, name="w2s", align_bytes=64)
-        warm = keep.tile([P, 2], F32, name="warm", align_bytes=64)
         ws = keep.tile([P, 2 * N], U8, name="ws", align_bytes=64)
         gw = [keep.tile([P, GATHER], U32, name=f"gw{g}", align_bytes=64) for g in range(S // GATHER)]
 
         nc.vector.memset(xs[:].bitcast(I32), 0)
-        nc.vector.memset(warm[:, 0:1], 0.0)
         nc.gpsimd.memset(ws[:].bitcast(I32), 0)
-        nc.scalar.activation(out=warm[:, 1:2], in_=warm[:, 0:1], func=GELU)
 
         w2v = w2.rearrange("(p j) c -> p j c", j=PACK)
-        nc.sync.dma_start(offsets[:], offs)
         nc.sync.dma_start(out=raw[0][:], in_=w2v[:, :, 0 : H // 2])
+        nc.sync.dma_start(offsets[:], offs)
         load_scales(nc.sync, xs, x_scales)
         nc.sync.dma_start(out=raw[1][:], in_=w2v[:, :, H // 2 : H])
         nc.sync.dma_start(out=xw[:].bitcast(I32), in_=words_of(x_words))
         load_scales(nc.gpsimd, ws[:, 0:N], w1_scales)
-        load_scales(nc.sync, ws[:, N : 2 * N], w3_scales)
+        load_scales(nc.gpsimd, ws[:, N : 2 * N], w3_scales, range(1))
+        load_scales(nc.sync, ws[:, N : 2 * N], w3_scales, range(1, 4))
 
         gs = {}
 
@@ -81,16 +79,14 @@ def tile_picked_lora_gelu_p_kernel(tc, x_words, x_scales, w1_words, w1_scales, w
 
         regroup(nc.scalar.copy, 0, 0, 64)
         regroup(nc.scalar.copy, 1, 0, SPLIT)
-        regroup(nc.vector.tensor_copy, 1, SPLIT, 64)
         ww = keep.tile([P, 2 * N], U32, name="ww", tag="raw1", align_bytes=64)
         nc.scalar.dma_start(out=ww[:, 0:N].bitcast(I32), in_=words_of(w1_words))
         nc.scalar.dma_start(out=ww[:, N : 2 * N].bitcast(I32), in_=words_of(w3_words))
         for t in range(PACK):
             cols = slice(t * P, (t + 1) * P)
             nc.vector.quantize_mx(out=w2w[:, cols].bitcast(FP8X4), scales=w2s[:, cols], in_=w2b[:, t].rearrange("p m j -> p (m j)"))
-        gather_scales(EARLY, S, "staged")
         scrap = psum.tile([P, P], F32, name="scrap", tag="bank7")
-        for r in range(12):
+        for r in range(9):
             nc.tensor.matmul_mx(out=scrap[:], lhsT=w2w[:, 0:P].bitcast(FP8X4), lhsT_scale=w2s[:, 0:P], rhs=w2w[:, 0:P].bitcast(FP8X4), rhs_scale=w2s[:, 0:P], start=True, stop=True)
         for g in range(S // GATHER):
             cols = slice(g * GATHER // 16, (g + 1) * GATHER // 16)
@@ -133,17 +129,24 @@ def tile_picked_lora_gelu_p_kernel(tc, x_words, x_scales, w1_words, w1_scales, w
             if last:
                 for m in range(2):
                     term(accs[m][:], m, 1)
+                return accs
+            acc = psum.tile([P, 2, width], F32, name="acc", tag=f"bank{(c + 4) % 8}")
+            for m in range(2):
+                term(acc[:, m, :], m, 0)
+                term(acc[:, m, :], m, 1)
+            return acc
+
+        def drain(c, n0, width, acc):
+            if c == len(CHUNKS) - 1:
+                accs = acc
                 res = [keep.tile([P, width], F32, name=f"resl{m}") for m in range(2)]
                 nc.scalar.copy(out=res[0][:], in_=accs[0][:])
                 nc.vector.tensor_copy(out=res[1][:], in_=accs[1][:])
                 nc.scalar.dma_start(out=out[0:P, n0 : n0 + width], in_=res[0][:])
                 nc.sync.dma_start(out=out[P : 2 * P, n0 : n0 + width], in_=res[1][:])
             else:
-                acc = psum.tile([P, 2, width], F32, name="acc", tag=f"bank{(c + 4) % 8}")
-                for m in range(2):
-                    term(acc[:, m, :], m, 0)
-                    term(acc[:, m, :], m, 1)
-                res = keep.tile([P, 2, width], F32, name=f"res{c}")
+                on_scalar = c >= len(CHUNKS) - 3
+                res = keep.tile([P, 2, width], F32, name=f"res{c}", tag=f"res{c}" if on_scalar else f"hb{c + 2}", align_bytes=64)
                 if c >= len(CHUNKS) - 3:
                     nc.scalar.copy(out=res[:], in_=acc[:])
                 else:
@@ -151,10 +154,12 @@ def tile_picked_lora_gelu_p_kernel(tc, x_words, x_scales, w1_words, w1_scales, w
                 nc.sync.dma_start(out=outv[:, :, n0 : n0 + width], in_=res[:])
 
         starts = [sum(CHUNKS[:c]) for c in range(len(CHUNKS))]
-        pending = None
-        for c, width in enumerate(CHUNKS):
-            hb = hidden(c, starts[c], width)
-            if pending is not None:
-                finish(*pending)
-            pending = (c, starts[c], width, hb)
-        finish(*pending)
+        staged = []
+        sums = []
+        for c in range(len(CHUNKS) + 5):
+            if c < len(CHUNKS):
+                staged.append(hidden(c, starts[c], CHUNKS[c]))
+            if 3 <= c < len(CHUNKS) + 3:
+                sums.append(finish(c - 3, starts[c - 3], CHUNKS[c - 3], staged[c - 3]))
+            if c >= 5:
+                drain(c - 5, starts[c - 5], CHUNKS[c - 5], sums[c - 5])

@@ -25,7 +25,7 @@ SPLIT = 64
 
 def load_scales(queue, plane, scales, quadrants=range(4)):
     for q in quadrants:
-        queue.dma_start(out=plane[32 * q : 32 * q + 4, :].bitcast(I32), in_=scales[0, 4 * q : 4 * q + 4, :].bitcast(I32))
+        queue.dma_start(out=plane[q:P:32, :].bitcast(I32), in_=scales[0, q:16:4, :].bitcast(I32))
 
 
 def words_of(dram):
@@ -45,11 +45,14 @@ def tile_picked_lora_gelu_p_kernel(tc, x_words, x_scales, w1_words, w1_scales, w
         w2b = keep.tile([P, PACK, P, PACK], BF16, name="w2b", tag="staged", align_bytes=64)
         w2w = keep.tile([P, H], U32, name="w2w", align_bytes=64)
         w2s = keep.tile([P, H], U8, name="w2s", align_bytes=64)
+        warm = keep.tile([P, 2], F32, name="warm", align_bytes=64)
         ws = keep.tile([P, 2 * N], U8, name="ws", align_bytes=64)
         gw = [keep.tile([P, GATHER], U32, name=f"gw{g}", align_bytes=64) for g in range(S // GATHER)]
 
         nc.vector.memset(xs[:].bitcast(I32), 0)
+        nc.vector.memset(warm[:, 0:1], 0.0)
         nc.gpsimd.memset(ws[:].bitcast(I32), 0)
+        nc.scalar.activation(out=warm[:, 1:2], in_=warm[:, 0:1], func=GELU)
 
         w2v = w2.rearrange("(p j) c -> p j c", j=PACK)
         nc.sync.dma_start(out=raw[0][:], in_=w2v[:, :, 0 : H // 2])
@@ -145,9 +148,9 @@ def tile_picked_lora_gelu_p_kernel(tc, x_words, x_scales, w1_words, w1_scales, w
                 nc.scalar.dma_start(out=out[0:P, n0 : n0 + width], in_=res[0][:])
                 nc.sync.dma_start(out=out[P : 2 * P, n0 : n0 + width], in_=res[1][:])
             else:
-                on_scalar = c >= len(CHUNKS) - 3
-                res = keep.tile([P, 2, width], F32, name=f"res{c}", tag=f"res{c}" if on_scalar else f"hb{c + 2}", align_bytes=64)
-                if c >= len(CHUNKS) - 3:
+                on_scalar = c >= len(CHUNKS) - 4
+                res = keep.tile([P, 2, width], F32, name=f"res{c}", tag=f"res{c}", align_bytes=64)
+                if c >= len(CHUNKS) - 4:
                     nc.scalar.copy(out=res[:], in_=acc[:])
                 else:
                     nc.vector.tensor_copy(out=res[:], in_=acc[:])

@@ -17,15 +17,20 @@ GELU = mybir.ActivationFunctionType.Gelu_apprx_tanh
 P = 128
 PACK = 4
 GATHER = 256
-SUB = 128
-CHUNKS = [128] * 8
-EARLY = 1024
-SPLIT = 64
+CHUNK = 128
+CHUNKS = S // CHUNK
+HALF = H // 2
+HALF_BYTES = PACK * HALF * 4
+VECTOR_SHARE = 32
+WARM_UP = [128,256,256,256,256]
+SCALAR_DRAINS = [5]
+PROJECT_LAG = 3
+DRAIN_LAG = 5
 
 
-def load_scales(queue, plane, scales, quadrants=range(4)):
-    for q in quadrants:
-        queue.dma_start(out=plane[q:P:32, :].bitcast(I32), in_=scales[0, q:16:4, :].bitcast(I32))
+def load_scales(queue, plane, scales):
+    for r in range(4):
+        queue.dma_start(out=plane[r:P:32, :].bitcast(I32), in_=scales[0, r:16:4, :].bitcast(I32))
 
 
 def words_of(dram):
@@ -36,43 +41,45 @@ def tile_picked_lora_gelu_p_kernel(tc, x_words, x_scales, w1_words, w1_scales, w
     nc = tc.nc
     with ExitStack() as ctx:
         keep = ctx.enter_context(tc.tile_pool(name="keep", bufs=1))
+        stage = ctx.enter_context(tc.tile_pool(name="stage", bufs=1))
         psum = ctx.enter_context(tc.psum_pool(name="psum", bufs=1))
 
         offsets = keep.tile([P, S // 16], U16, name="offsets")
-        xs = keep.tile([P, T], U8, name="xs", align_bytes=64)
+        xs = keep.tile([P, T], U8, name="xs", tag="scale_rows", align_bytes=64)
         xw = keep.tile([P, T], U32, name="xw", align_bytes=64)
-        raw = [keep.tile([P, PACK, H // 2], F32, name=f"raw{a}", tag=f"raw{a}", align_bytes=64) for a in range(2)]
-        w2b = keep.tile([P, PACK, P, PACK], BF16, name="w2b", tag="staged", align_bytes=64)
+        raw = [stage.tile([P, PACK, HALF], F32, name=f"raw{a}", offset=a * HALF_BYTES, align_bytes=64) for a in range(2)]
+        w2b = keep.tile([P, PACK, P, PACK], BF16, name="w2b", align_bytes=64)
         w2w = keep.tile([P, H], U32, name="w2w", align_bytes=64)
         w2s = keep.tile([P, H], U8, name="w2s", align_bytes=64)
         warm = keep.tile([P, 2], F32, name="warm", align_bytes=64)
-        ws = keep.tile([P, 2 * N], U8, name="ws", align_bytes=64)
+        picked = keep.tile([P, S], U8, name="picked", align_bytes=64)
+        gs = keep.tile([P, S], U8, name="gs", align_bytes=64)
+        w1s = keep.tile([P, N], U8, name="w1s", align_bytes=64)
         gw = [keep.tile([P, GATHER], U32, name=f"gw{g}", align_bytes=64) for g in range(S // GATHER)]
 
-        nc.vector.memset(xs[:].bitcast(I32), 0)
         nc.vector.memset(warm[:, 0:1], 0.0)
-        nc.gpsimd.memset(ws[:].bitcast(I32), 0)
+        for rows in (slice(0, 16), slice(32, 64), slice(64, P)):
+            nc.vector.memset(xs[rows, :].bitcast(I32), 0)
+        nc.vector.memset(gs[:].bitcast(I32), 0)
+        nc.gpsimd.memset(w1s[:].bitcast(I32), 0)
         nc.scalar.activation(out=warm[:, 1:2], in_=warm[:, 0:1], func=GELU)
 
         w2v = w2.rearrange("(p j) c -> p j c", j=PACK)
-        nc.sync.dma_start(out=raw[0][:], in_=w2v[:, :, 0 : H // 2])
         nc.sync.dma_start(offsets[:], offs)
-        load_scales(nc.sync, xs, x_scales)
-        nc.sync.dma_start(out=raw[1][:], in_=w2v[:, :, H // 2 : H])
+        nc.sync.dma_start(out=xs[16:32, :].bitcast(I32), in_=x_scales[0].bitcast(I32))
+        nc.sync.dma_start(out=raw[0][:], in_=w2v[:, :, 0:HALF])
+        nc.sync.dma_start(out=raw[1][:], in_=w2v[:, :, HALF:H])
         nc.sync.dma_start(out=xw[:].bitcast(I32), in_=words_of(x_words))
-        load_scales(nc.gpsimd, ws[:, 0:N], w1_scales)
-        load_scales(nc.gpsimd, ws[:, N : 2 * N], w3_scales, range(1))
-        load_scales(nc.sync, ws[:, N : 2 * N], w3_scales, range(1, 4))
+        load_scales(nc.gpsimd, w1s, w1_scales)
 
-        gs = {}
-
-        def gather_scales(n0, n1, tag):
-            tile = keep.tile([P, n1 - n0], U8, name=f"gs{n0}", tag=tag, align_bytes=64)
-            nc.vector.tensor_copy(tile[:], xs[:].indirect(offsets[:, n0 // 16 : n1 // 16]))
-            for n in range(n0, n1, SUB):
-                gs[n] = (tile, n0)
-
-        gather_scales(0, EARLY, "gs_early")
+        nc.vector.tensor_copy(picked[:], xs[:].indirect(offsets[:]))
+        ww = keep.tile([P, 2 * N], U32, name="ww", tag="scale_rows", align_bytes=64)
+        w1w = ww[:, 0:N]
+        w3w = ww[:, N : 2 * N]
+        for r in range(4):
+            nc.sync.dma_start(out=gs[r:P:32, :].bitcast(I32), in_=picked[16 + r : 32 : 4, :].bitcast(I32))
+        nc.sync.dma_start(out=w1w.bitcast(I32), in_=words_of(w1_words))
+        nc.sync.dma_start(out=w3w.bitcast(I32), in_=words_of(w3_words))
 
         def regroup(copy, a, m0, m1):
             copy(
@@ -81,88 +88,89 @@ def tile_picked_lora_gelu_p_kernel(tc, x_words, x_scales, w1_words, w1_scales, w
             )
 
         regroup(nc.scalar.copy, 0, 0, 64)
-        regroup(nc.scalar.copy, 1, 0, SPLIT)
-        ww = keep.tile([P, 2 * N], U32, name="ww", tag="raw1", align_bytes=64)
-        nc.scalar.dma_start(out=ww[:, 0:N].bitcast(I32), in_=words_of(w1_words))
-        nc.scalar.dma_start(out=ww[:, N : 2 * N].bitcast(I32), in_=words_of(w3_words))
+        regroup(nc.scalar.copy, 1, 0, 64 - VECTOR_SHARE)
+        w3s = stage.tile([P, N], U8, name="w3s", offset=0, align_bytes=64)
+        nc.vector.memset(w3s[:].bitcast(I32), 0)
+        load_scales(nc.scalar, w3s, w3_scales)
+        regroup(nc.vector.tensor_copy, 1, 64 - VECTOR_SHARE, 64)
         for t in range(PACK):
             cols = slice(t * P, (t + 1) * P)
             nc.vector.quantize_mx(out=w2w[:, cols].bitcast(FP8X4), scales=w2s[:, cols], in_=w2b[:, t].rearrange("p m j -> p (m j)"))
-        scrap = psum.tile([P, P], F32, name="scrap", tag="bank7")
-        for r in range(9):
-            nc.tensor.matmul_mx(out=scrap[:], lhsT=w2w[:, 0:P].bitcast(FP8X4), lhsT_scale=w2s[:, 0:P], rhs=w2w[:, 0:P].bitcast(FP8X4), rhs_scale=w2s[:, 0:P], start=True, stop=True)
+        scrap = psum.tile([P, 2 * P], F32, name="scrap", tag="bank7")
+        for width in WARM_UP:
+            nc.tensor.matmul_mx(out=scrap[:, 0:width], lhsT=w2w[:, 0:P].bitcast(FP8X4), lhsT_scale=w2s[:, 0:P], rhs=w2w[:, 0:width].bitcast(FP8X4), rhs_scale=w2s[:, 0:width], start=True, stop=True)
         for g in range(S // GATHER):
             cols = slice(g * GATHER // 16, (g + 1) * GATHER // 16)
             nc.vector.tensor_copy(gw[g][:], xw[:].indirect(offsets[:, cols]))
 
-        def x_operand(n0, width):
-            g, o = divmod(n0, GATHER)
-            tile, first = gs[n0]
-            return gw[g][:, o : o + width].bitcast(FP8X4), tile[:, n0 - first : n0 - first + width]
+        def x_operand(c):
+            g, o = divmod(c * CHUNK, GATHER)
+            n0 = c * CHUNK
+            scales = gs[:, n0 : n0 + CHUNK]
+            return gw[g][:, o : o + CHUNK].bitcast(FP8X4), scales
 
         outv = out.rearrange("(m p) n -> p m n", p=P)
 
-        def hidden(c, n0, width):
-            hb = keep.tile([P, width, PACK], BF16, name=f"hb{c}", tag=f"hb{c}", align_bytes=64)
-            for s0 in range(0, width, SUB):
-                hp = psum.tile([P, PACK, SUB], F32, name="hp", tag=f"bank{(n0 + s0) // SUB % 4}")
-                xq, xsc = x_operand(n0 + s0, SUB)
-                for t in range(PACK):
-                    cols = slice(t * P, (t + 1) * P)
-                    nc.tensor.matmul_mx(out=hp[:, t, :], lhsT=w2w[:, cols].bitcast(FP8X4), lhsT_scale=w2s[:, cols], rhs=xq, rhs_scale=xsc, start=True, stop=True)
-                nc.scalar.activation(out=hb[:, s0 : s0 + SUB, :], in_=hp[:].rearrange("p t n -> p n t"), func=GELU)
+        def hidden(c):
+            hb = keep.tile([P, CHUNK, PACK], BF16, name=f"hb{c}", align_bytes=64)
+            hp = psum.tile([P, PACK, CHUNK], F32, name="hp", tag=f"bank{c % 4}")
+            xq, xsc = x_operand(c)
+            for t in range(PACK):
+                cols = slice(t * P, (t + 1) * P)
+                nc.tensor.matmul_mx(out=hp[:, t, :], lhsT=w2w[:, cols].bitcast(FP8X4), lhsT_scale=w2s[:, cols], rhs=xq, rhs_scale=xsc, start=True, stop=True)
+            nc.scalar.activation(out=hb[:], in_=hp[:].rearrange("p t n -> p n t"), func=GELU)
             return hb
 
-        def finish(c, n0, width, hb):
-            last = c == len(CHUNKS) - 1
-            hw = keep.tile([P, width], U32, name=f"hw{c}", align_bytes=64)
-            hs = keep.tile([P, width], U8, name=f"hs{c}", align_bytes=64)
-            xq, xsc = x_operand(n0, width)
+        def project(c, hb):
+            hw = keep.tile([P, CHUNK], U32, name=f"hw{c}", align_bytes=64)
+            hs = keep.tile([P, CHUNK], U8, name=f"hs{c}", align_bytes=64)
+            xq, xsc = x_operand(c)
 
-            def term(dst, m, second):
-                cols = slice(second * N + m * P, second * N + (m + 1) * P)
-                rhs, rsc = (hw[:].bitcast(FP8X4), hs[:]) if second else (xq, xsc)
-                nc.tensor.matmul_mx(out=dst, lhsT=ww[:, cols].bitcast(FP8X4), lhsT_scale=ws[:, cols], rhs=rhs, rhs_scale=rsc, start=not second, stop=bool(second))
+            def own_term(dst, m):
+                cols = slice(m * P, (m + 1) * P)
+                nc.tensor.matmul_mx(out=dst, lhsT=w1w[:, cols].bitcast(FP8X4), lhsT_scale=w1s[:, cols], rhs=xq, rhs_scale=xsc, start=True, stop=False)
 
-            if last:
-                accs = [psum.tile([P, width], F32, name=f"last{m}", tag=f"bank{(c + m + 4) % 8}") for m in range(2)]
+            def adapter_term(dst, m):
+                cols = slice(m * P, (m + 1) * P)
+                nc.tensor.matmul_mx(out=dst, lhsT=w3w[:, cols].bitcast(FP8X4), lhsT_scale=w3s[:, cols], rhs=hw[:].bitcast(FP8X4), rhs_scale=hs[:], start=False, stop=True)
+
+            if c == CHUNKS - 1:
+                accs = [psum.tile([P, CHUNK], F32, name=f"last{m}", tag=f"bank{(c + m + 4) % 8}") for m in range(2)]
                 for m in range(2):
-                    term(accs[m][:], m, 0)
+                    own_term(accs[m][:], m)
             nc.vector.quantize_mx(out=hw[:].bitcast(FP8X4), scales=hs[:], in_=hb[:].rearrange("p n t -> p (n t)"))
-            if last:
+            if c == CHUNKS - 1:
                 for m in range(2):
-                    term(accs[m][:], m, 1)
+                    adapter_term(accs[m][:], m)
                 return accs
-            acc = psum.tile([P, 2, width], F32, name="acc", tag=f"bank{(c + 4) % 8}")
+            acc = psum.tile([P, 2, CHUNK], F32, name="acc", tag=f"bank{(c + 4) % 8}")
             for m in range(2):
-                term(acc[:, m, :], m, 0)
-                term(acc[:, m, :], m, 1)
+                own_term(acc[:, m, :], m)
+                adapter_term(acc[:, m, :], m)
             return acc
 
-        def drain(c, n0, width, acc):
-            if c == len(CHUNKS) - 1:
-                accs = acc
-                res = [keep.tile([P, width], F32, name=f"resl{m}") for m in range(2)]
-                nc.scalar.copy(out=res[0][:], in_=accs[0][:])
-                nc.vector.tensor_copy(out=res[1][:], in_=accs[1][:])
-                nc.scalar.dma_start(out=out[0:P, n0 : n0 + width], in_=res[0][:])
-                nc.sync.dma_start(out=out[P : 2 * P, n0 : n0 + width], in_=res[1][:])
+        def drain(c, acc):
+            cols = slice(c * CHUNK, (c + 1) * CHUNK)
+            if c == CHUNKS - 1:
+                res = [keep.tile([P, CHUNK], F32, name=f"last_res{m}", align_bytes=64) for m in range(2)]
+                nc.scalar.copy(out=res[0][:], in_=acc[0][:])
+                nc.vector.tensor_copy(out=res[1][:], in_=acc[1][:])
+                nc.scalar.dma_start(out=out[0:P, cols], in_=res[0][:])
+                nc.sync.dma_start(out=out[P : 2 * P, cols], in_=res[1][:])
+                return
+            res = keep.tile([P, 2, CHUNK], F32, name=f"res{c}", align_bytes=64)
+            if c in SCALAR_DRAINS:
+                nc.scalar.copy(out=res[:], in_=acc[:])
             else:
-                on_scalar = c >= len(CHUNKS) - 4
-                res = keep.tile([P, 2, width], F32, name=f"res{c}", tag=f"res{c}", align_bytes=64)
-                if c >= len(CHUNKS) - 4:
-                    nc.scalar.copy(out=res[:], in_=acc[:])
-                else:
-                    nc.vector.tensor_copy(out=res[:], in_=acc[:])
-                nc.sync.dma_start(out=outv[:, :, n0 : n0 + width], in_=res[:])
+                nc.vector.tensor_copy(out=res[:], in_=acc[:])
+            nc.sync.dma_start(out=outv[:, :, cols], in_=res[:])
 
-        starts = [sum(CHUNKS[:c]) for c in range(len(CHUNKS))]
         staged = []
         sums = []
-        for c in range(len(CHUNKS) + 5):
-            if c < len(CHUNKS):
-                staged.append(hidden(c, starts[c], CHUNKS[c]))
-            if 3 <= c < len(CHUNKS) + 3:
-                sums.append(finish(c - 3, starts[c - 3], CHUNKS[c - 3], staged[c - 3]))
-            if c >= 5:
-                drain(c - 5, starts[c - 5], CHUNKS[c - 5], sums[c - 5])
+        for step in range(CHUNKS + DRAIN_LAG):
+            if step < CHUNKS:
+                staged.append(hidden(step))
+            if 0 <= step - PROJECT_LAG < CHUNKS:
+                sums.append(project(step - PROJECT_LAG, staged[step - PROJECT_LAG]))
+            if step >= DRAIN_LAG:
+                drain(step - DRAIN_LAG, sums[step - DRAIN_LAG])

@@ -20,17 +20,14 @@ GATHER = 256
 CHUNK = 128
 CHUNKS = S // CHUNK
 HALF = H // 2
-HALF_BYTES = PACK * HALF * 4
-VECTOR_SHARE = 32
+SCALAR_SHARE = 32
 WARM_UP = [128,256,256,256,256]
 SCALAR_DRAINS = [5]
+PIECES = [(c * CHUNK, (c + 1) * CHUNK) for c in range(CHUNKS)]
+OUT_BANKS = [(4,), (5,), (6,), (7,), (4,), (5,), (6, 0), (1, 7)]
+STORE_FROM = {1: 0, 3: 2, 4: 4, 5: 5, 6: 6}
 PROJECT_LAG = 3
 DRAIN_LAG = 5
-
-
-def load_scales(queue, plane, scales):
-    for r in range(4):
-        queue.dma_start(out=plane[r:P:32, :].bitcast(I32), in_=scales[0, r:16:4, :].bitcast(I32))
 
 
 def words_of(dram):
@@ -47,37 +44,44 @@ def tile_picked_lora_gelu_p_kernel(tc, x_words, x_scales, w1_words, w1_scales, w
         offsets = keep.tile([P, S // 16], U16, name="offsets")
         xs = keep.tile([P, T], U8, name="xs", tag="scale_rows", align_bytes=64)
         xw = keep.tile([P, T], U32, name="xw", align_bytes=64)
-        raw = [stage.tile([P, PACK, HALF], F32, name=f"raw{a}", offset=a * HALF_BYTES, align_bytes=64) for a in range(2)]
+        raw = [stage.tile([P, PACK, HALF], F32, name=f"raw{a}", offset=a * PACK * HALF * 4, align_bytes=64) for a in range(2)]
         w2b = keep.tile([P, PACK, P, PACK], BF16, name="w2b", align_bytes=64)
         w2w = keep.tile([P, H], U32, name="w2w", align_bytes=64)
         w2s = keep.tile([P, H], U8, name="w2s", align_bytes=64)
         warm = keep.tile([P, 2], F32, name="warm", align_bytes=64)
-        picked = keep.tile([P, S], U8, name="picked", align_bytes=64)
         gs = keep.tile([P, S], U8, name="gs", align_bytes=64)
-        w1s = keep.tile([P, N], U8, name="w1s", align_bytes=64)
+        staged_rows = keep.tile([P, 2 * N], U8, name="staged_rows", align_bytes=64)
+        ws = keep.tile([P, 2 * N], U8, name="ws", align_bytes=64)
+        w1s = ws[:, 0:N]
+        w3s = ws[:, N : 2 * N]
+        picked = keep.tile([P, S], U8, name="picked", align_bytes=64)
         gw = [keep.tile([P, GATHER], U32, name=f"gw{g}", align_bytes=64) for g in range(S // GATHER)]
 
         nc.vector.memset(warm[:, 0:1], 0.0)
         for rows in (slice(0, 16), slice(32, 64), slice(64, P)):
             nc.vector.memset(xs[rows, :].bitcast(I32), 0)
         nc.vector.memset(gs[:].bitcast(I32), 0)
-        nc.gpsimd.memset(w1s[:].bitcast(I32), 0)
+        nc.vector.memset(ws[:].bitcast(I32), 0)
         nc.scalar.activation(out=warm[:, 1:2], in_=warm[:, 0:1], func=GELU)
 
         w2v = w2.rearrange("(p j) c -> p j c", j=PACK)
         nc.sync.dma_start(offsets[:], offs)
         nc.sync.dma_start(out=xs[16:32, :].bitcast(I32), in_=x_scales[0].bitcast(I32))
-        nc.sync.dma_start(out=raw[0][:], in_=w2v[:, :, 0:HALF])
-        nc.sync.dma_start(out=raw[1][:], in_=w2v[:, :, HALF:H])
+        for a in range(2):
+            nc.sync.dma_start(out=raw[a][:], in_=w2v[:, :, a * HALF : (a + 1) * HALF])
         nc.sync.dma_start(out=xw[:].bitcast(I32), in_=words_of(x_words))
-        load_scales(nc.gpsimd, w1s, w1_scales)
+        nc.sync.dma_start(out=staged_rows[16:32, 0:N].bitcast(I32), in_=w1_scales[0].bitcast(I32))
+        nc.sync.dma_start(out=staged_rows[16:32, N : 2 * N].bitcast(I32), in_=w3_scales[0].bitcast(I32))
+
+        def place_scales(queue, plane, rows):
+            for r in range(4):
+                queue.dma_start(out=plane[r:P:32, :].bitcast(I32), in_=rows[16 + r : 32 : 4, :].bitcast(I32))
 
         nc.vector.tensor_copy(picked[:], xs[:].indirect(offsets[:]))
         ww = keep.tile([P, 2 * N], U32, name="ww", tag="scale_rows", align_bytes=64)
         w1w = ww[:, 0:N]
         w3w = ww[:, N : 2 * N]
-        for r in range(4):
-            nc.sync.dma_start(out=gs[r:P:32, :].bitcast(I32), in_=picked[16 + r : 32 : 4, :].bitcast(I32))
+        place_scales(nc.sync, gs, picked)
         nc.sync.dma_start(out=w1w.bitcast(I32), in_=words_of(w1_words))
         nc.sync.dma_start(out=w3w.bitcast(I32), in_=words_of(w3_words))
 
@@ -88,89 +92,99 @@ def tile_picked_lora_gelu_p_kernel(tc, x_words, x_scales, w1_words, w1_scales, w
             )
 
         regroup(nc.scalar.copy, 0, 0, 64)
-        regroup(nc.scalar.copy, 1, 0, 64 - VECTOR_SHARE)
-        w3s = stage.tile([P, N], U8, name="w3s", offset=0, align_bytes=64)
-        nc.vector.memset(w3s[:].bitcast(I32), 0)
-        load_scales(nc.scalar, w3s, w3_scales)
-        regroup(nc.vector.tensor_copy, 1, 64 - VECTOR_SHARE, 64)
+        regroup(nc.scalar.copy, 1, 0, SCALAR_SHARE)
+        regroup(nc.vector.tensor_copy, 1, SCALAR_SHARE, 64)
+        place_scales(nc.scalar, ws, staged_rows)
         for t in range(PACK):
             cols = slice(t * P, (t + 1) * P)
             nc.vector.quantize_mx(out=w2w[:, cols].bitcast(FP8X4), scales=w2s[:, cols], in_=w2b[:, t].rearrange("p m j -> p (m j)"))
-        scrap = psum.tile([P, 2 * P], F32, name="scrap", tag="bank7")
+        scrap = psum.tile([P, 4 * P], F32, name="scrap", tag="bank7")
         for width in WARM_UP:
             nc.tensor.matmul_mx(out=scrap[:, 0:width], lhsT=w2w[:, 0:P].bitcast(FP8X4), lhsT_scale=w2s[:, 0:P], rhs=w2w[:, 0:width].bitcast(FP8X4), rhs_scale=w2s[:, 0:width], start=True, stop=True)
         for g in range(S // GATHER):
             cols = slice(g * GATHER // 16, (g + 1) * GATHER // 16)
             nc.vector.tensor_copy(gw[g][:], xw[:].indirect(offsets[:, cols]))
 
-        def x_operand(c):
-            g, o = divmod(c * CHUNK, GATHER)
-            n0 = c * CHUNK
-            scales = gs[:, n0 : n0 + CHUNK]
-            return gw[g][:, o : o + CHUNK].bitcast(FP8X4), scales
-
         outv = out.rearrange("(m p) n -> p m n", p=P)
+        hw = keep.tile([P, S], U32, name="hw", align_bytes=64)
+        hs = keep.tile([P, S], U8, name="hs", align_bytes=64)
+
+        def x_operand(n0):
+            g, o = divmod(n0, GATHER)
+            return gw[g][:, o : o + CHUNK].bitcast(FP8X4), gs[:, n0 : n0 + CHUNK]
 
         def hidden(c):
-            hb = keep.tile([P, CHUNK, PACK], BF16, name=f"hb{c}", align_bytes=64)
             hp = psum.tile([P, PACK, CHUNK], F32, name="hp", tag=f"bank{c % 4}")
-            xq, xsc = x_operand(c)
+            xq, xsc = x_operand(c * CHUNK)
             for t in range(PACK):
                 cols = slice(t * P, (t + 1) * P)
                 nc.tensor.matmul_mx(out=hp[:, t, :], lhsT=w2w[:, cols].bitcast(FP8X4), lhsT_scale=w2s[:, cols], rhs=xq, rhs_scale=xsc, start=True, stop=True)
-            nc.scalar.activation(out=hb[:], in_=hp[:].rearrange("p t n -> p n t"), func=GELU)
-            return hb
+            return hp
 
-        def project(c, hb):
-            hw = keep.tile([P, CHUNK], U32, name=f"hw{c}", align_bytes=64)
-            hs = keep.tile([P, CHUNK], U8, name=f"hs{c}", align_bytes=64)
-            xq, xsc = x_operand(c)
+        def activate(hp, a, b):
+            hb = keep.tile([P, b - a, PACK], BF16, name=f"hb{len(staged)}", align_bytes=64)
+            nc.scalar.activation(out=hb[:], in_=hp[:, :, a:b].rearrange("p t n -> p n t"), func=GELU)
+            staged.append(hb)
 
-            def own_term(dst, m):
-                cols = slice(m * P, (m + 1) * P)
-                nc.tensor.matmul_mx(out=dst, lhsT=w1w[:, cols].bitcast(FP8X4), lhsT_scale=w1s[:, cols], rhs=xq, rhs_scale=xsc, start=True, stop=False)
+        def own_term(dst, m, n0):
+            cols = slice(m * P, (m + 1) * P)
+            xq, xsc = x_operand(n0)
+            nc.tensor.matmul_mx(out=dst, lhsT=w1w[:, cols].bitcast(FP8X4), lhsT_scale=w1s[:, cols], rhs=xq, rhs_scale=xsc, start=True, stop=False)
 
-            def adapter_term(dst, m):
-                cols = slice(m * P, (m + 1) * P)
-                nc.tensor.matmul_mx(out=dst, lhsT=w3w[:, cols].bitcast(FP8X4), lhsT_scale=w3s[:, cols], rhs=hw[:].bitcast(FP8X4), rhs_scale=hs[:], start=False, stop=True)
+        def adapter_term(dst, m, n0):
+            cols = slice(m * P, (m + 1) * P)
+            nc.tensor.matmul_mx(out=dst, lhsT=w3w[:, cols].bitcast(FP8X4), lhsT_scale=w3s[:, cols], rhs=hw[:, n0 : n0 + CHUNK].bitcast(FP8X4), rhs_scale=hs[:, n0 : n0 + CHUNK], start=False, stop=True)
 
-            if c == CHUNKS - 1:
-                accs = [psum.tile([P, CHUNK], F32, name=f"last{m}", tag=f"bank{(c + m + 4) % 8}") for m in range(2)]
+        def project(u):
+            first, last = PIECES[u]
+            n0 = last - CHUNK
+            banks = OUT_BANKS[u]
+            if len(banks) == 2:
+                accs = [psum.tile([P, CHUNK], F32, name=f"half{m}", tag=f"bank{banks[m]}") for m in range(2)]
                 for m in range(2):
-                    own_term(accs[m][:], m)
-            nc.vector.quantize_mx(out=hw[:].bitcast(FP8X4), scales=hs[:], in_=hb[:].rearrange("p n t -> p (n t)"))
-            if c == CHUNKS - 1:
+                    own_term(accs[m][:], m, n0)
+            nc.vector.quantize_mx(out=hw[:, first:last].bitcast(FP8X4), scales=hs[:, first:last], in_=staged[u][:].rearrange("p n t -> p (n t)"))
+            if len(banks) == 2:
                 for m in range(2):
-                    adapter_term(accs[m][:], m)
+                    adapter_term(accs[m][:], m, n0)
                 return accs
-            acc = psum.tile([P, 2, CHUNK], F32, name="acc", tag=f"bank{(c + 4) % 8}")
+            acc = psum.tile([P, 2, CHUNK], F32, name="acc", tag=f"bank{banks[0]}")
             for m in range(2):
-                own_term(acc[:, m, :], m)
-                adapter_term(acc[:, m, :], m)
+                own_term(acc[:, m, :], m, n0)
+                adapter_term(acc[:, m, :], m, n0)
             return acc
 
-        def drain(c, acc):
-            cols = slice(c * CHUNK, (c + 1) * CHUNK)
-            if c == CHUNKS - 1:
+        def drain(u, acc):
+            first, last = PIECES[u]
+            if u == len(PIECES) - 1:
                 res = [keep.tile([P, CHUNK], F32, name=f"last_res{m}", align_bytes=64) for m in range(2)]
                 nc.scalar.copy(out=res[0][:], in_=acc[0][:])
                 nc.vector.tensor_copy(out=res[1][:], in_=acc[1][:])
-                nc.scalar.dma_start(out=out[0:P, cols], in_=res[0][:])
-                nc.sync.dma_start(out=out[P : 2 * P, cols], in_=res[1][:])
+                nc.scalar.dma_start(out=out[0:P, first:last], in_=res[0][:])
+                nc.sync.dma_start(out=out[P : 2 * P, first:last], in_=res[1][:])
                 return
-            res = keep.tile([P, 2, CHUNK], F32, name=f"res{c}", align_bytes=64)
-            if c in SCALAR_DRAINS:
-                nc.scalar.copy(out=res[:], in_=acc[:])
+            res = results[:, :, first:last]
+            if len(OUT_BANKS[u]) == 2:
+                nc.scalar.copy(out=res[:, 0, :], in_=acc[0][:])
+                nc.vector.tensor_copy(out=res[:, 1, :], in_=acc[1][:])
+            elif u in SCALAR_DRAINS:
+                nc.scalar.copy(out=res, in_=acc[:])
             else:
-                nc.vector.tensor_copy(out=res[:], in_=acc[:])
-            nc.sync.dma_start(out=outv[:, :, cols], in_=res[:])
+                nc.vector.tensor_copy(out=res, in_=acc[:])
+            if u in STORE_FROM:
+                cols = slice(STORE_FROM[u] * CHUNK, last)
+                nc.sync.dma_start(out=outv[:, :, cols], in_=results[:, :, cols])
 
+        results = keep.tile([P, 2, S - CHUNK], F32, name="results", align_bytes=64)
         staged = []
         sums = []
-        for step in range(CHUNKS + DRAIN_LAG):
+        for step in range(len(PIECES) + DRAIN_LAG):
             if step < CHUNKS:
-                staged.append(hidden(step))
-            if 0 <= step - PROJECT_LAG < CHUNKS:
-                sums.append(project(step - PROJECT_LAG, staged[step - PROJECT_LAG]))
+                hp = hidden(step)
+                for first, last in PIECES:
+                    if first // CHUNK == step:
+                        activate(hp, first - step * CHUNK, last - step * CHUNK)
+            if 0 <= step - PROJECT_LAG < len(PIECES):
+                sums.append(project(step - PROJECT_LAG))
             if step >= DRAIN_LAG:
                 drain(step - DRAIN_LAG, sums[step - DRAIN_LAG])

@@ -20,7 +20,7 @@ GATHER = 256
 CHUNK = 128
 CHUNKS = S // CHUNK
 HALF = H // 2
-SCALAR_SHARE = 32
+SCALAR_SHARE = 26
 WARM_UP = [128,256,256,256,256]
 SCALAR_DRAINS = [5]
 PIECES = [(c * CHUNK, (c + 1) * CHUNK) for c in range(CHUNKS)]
@@ -49,19 +49,18 @@ def tile_picked_lora_gelu_p_kernel(tc, x_words, x_scales, w1_words, w1_scales, w
         w2w = keep.tile([P, H], U32, name="w2w", align_bytes=64)
         w2s = keep.tile([P, H], U8, name="w2s", align_bytes=64)
         warm = keep.tile([P, 2], F32, name="warm", align_bytes=64)
-        gs = keep.tile([P, S], U8, name="gs", align_bytes=64)
-        staged_rows = keep.tile([P, 2 * N], U8, name="staged_rows", align_bytes=64)
-        ws = keep.tile([P, 2 * N], U8, name="ws", align_bytes=64)
-        w1s = ws[:, 0:N]
-        w3s = ws[:, N : 2 * N]
-        picked = keep.tile([P, S], U8, name="picked", align_bytes=64)
+        early_plane = keep.tile([P, S // 2], U8, name="early_plane", align_bytes=64)
+        late_planes = keep.tile([P, S // 2 + 2 * N], U8, name="late_planes", align_bytes=64)
+        w1s = late_planes[:, S // 2 : S // 2 + N]
+        w3s = late_planes[:, S // 2 + N : S // 2 + 2 * N]
+        picked = [keep.tile([P, S // 2], U8, name=f"picked{a}", align_bytes=64) for a in range(2)]
         gw = [keep.tile([P, GATHER], U32, name=f"gw{g}", align_bytes=64) for g in range(S // GATHER)]
 
         nc.vector.memset(warm[:, 0:1], 0.0)
         for rows in (slice(0, 16), slice(32, 64), slice(64, P)):
             nc.vector.memset(xs[rows, :].bitcast(I32), 0)
-        nc.vector.memset(gs[:].bitcast(I32), 0)
-        nc.vector.memset(ws[:].bitcast(I32), 0)
+        nc.vector.memset(early_plane[:].bitcast(I32), 0)
+        nc.vector.memset(late_planes[:].bitcast(I32), 0)
         nc.scalar.activation(out=warm[:, 1:2], in_=warm[:, 0:1], func=GELU)
 
         w2v = w2.rearrange("(p j) c -> p j c", j=PACK)
@@ -70,18 +69,17 @@ def tile_picked_lora_gelu_p_kernel(tc, x_words, x_scales, w1_words, w1_scales, w
         for a in range(2):
             nc.sync.dma_start(out=raw[a][:], in_=w2v[:, :, a * HALF : (a + 1) * HALF])
         nc.sync.dma_start(out=xw[:].bitcast(I32), in_=words_of(x_words))
-        nc.sync.dma_start(out=staged_rows[16:32, 0:N].bitcast(I32), in_=w1_scales[0].bitcast(I32))
-        nc.sync.dma_start(out=staged_rows[16:32, N : 2 * N].bitcast(I32), in_=w3_scales[0].bitcast(I32))
 
         def place_scales(queue, plane, rows):
             for r in range(4):
                 queue.dma_start(out=plane[r:P:32, :].bitcast(I32), in_=rows[16 + r : 32 : 4, :].bitcast(I32))
 
-        nc.vector.tensor_copy(picked[:], xs[:].indirect(offsets[:]))
+        for a in range(2):
+            nc.vector.tensor_copy(picked[a][:], xs[:].indirect(offsets[:, a * S // 32 : (a + 1) * S // 32]))
         ww = keep.tile([P, 2 * N], U32, name="ww", tag="scale_rows", align_bytes=64)
         w1w = ww[:, 0:N]
         w3w = ww[:, N : 2 * N]
-        place_scales(nc.sync, gs, picked)
+        place_scales(nc.sync, early_plane, picked[0])
         nc.sync.dma_start(out=w1w.bitcast(I32), in_=words_of(w1_words))
         nc.sync.dma_start(out=w3w.bitcast(I32), in_=words_of(w3_words))
 
@@ -92,9 +90,14 @@ def tile_picked_lora_gelu_p_kernel(tc, x_words, x_scales, w1_words, w1_scales, w
             )
 
         regroup(nc.scalar.copy, 0, 0, 64)
+        late_rows = stage.tile([P, S // 2 + 2 * N], U8, name="late_rows", offset=0, align_bytes=64)
+        nc.scalar.dma_start(out=late_rows[16:32, S // 2 : S // 2 + N].bitcast(I32), in_=w1_scales[0].bitcast(I32))
+        nc.scalar.dma_start(out=late_rows[16:32, S // 2 + N : S // 2 + 2 * N].bitcast(I32), in_=w3_scales[0].bitcast(I32))
         regroup(nc.scalar.copy, 1, 0, SCALAR_SHARE)
+        nc.vector.tensor_copy(out=late_rows[:, 0 : S // 2].bitcast(I32), in_=picked[1][:].bitcast(I32))
         regroup(nc.vector.tensor_copy, 1, SCALAR_SHARE, 64)
-        place_scales(nc.scalar, ws, staged_rows)
+        place_scales(nc.scalar, late_planes, late_rows)
+        gs = [early_plane, late_planes]
         for t in range(PACK):
             cols = slice(t * P, (t + 1) * P)
             nc.vector.quantize_mx(out=w2w[:, cols].bitcast(FP8X4), scales=w2s[:, cols], in_=w2b[:, t].rearrange("p m j -> p (m j)"))
@@ -111,7 +114,7 @@ def tile_picked_lora_gelu_p_kernel(tc, x_words, x_scales, w1_words, w1_scales, w
 
         def x_operand(n0):
             g, o = divmod(n0, GATHER)
-            return gw[g][:, o : o + CHUNK].bitcast(FP8X4), gs[:, n0 : n0 + CHUNK]
+            return gw[g][:, o : o + CHUNK].bitcast(FP8X4), gs[n0 // (S // 2)][:, n0 % (S // 2) : n0 % (S // 2) + CHUNK]
 
         def hidden(c):
             hp = psum.tile([P, PACK, CHUNK], F32, name="hp", tag=f"bank{c % 4}")

@@ -16,15 +16,20 @@ GELU = mybir.ActivationFunctionType.Gelu_apprx_tanh
 
 P = 128
 PACK = 4
+LIST_ROWS = 16
+BLOCKS = 16
+STAGED = slice(16, 16 + BLOCKS)
 GATHER = 256
 CHUNK = 128
 CHUNKS = S // CHUNK
-HALF = H // 2
-SCALAR_SHARE = 26
-WARM_UP = [128,256,256,256,256]
-SCALAR_DRAINS = [5]
-PIECES = [(c * CHUNK, (c + 1) * CHUNK) for c in range(CHUNKS)]
+HALF_TOKENS = S // 2
+HALF_H = H // 2
+GROUPS = HALF_H // PACK
+SCALAR_GROUPS = 26
+WARM_UP = [128, 256, 256, 256, 256]
+H_BANKS = 4
 OUT_BANKS = [(4,), (5,), (6,), (7,), (4,), (5,), (6, 0), (1, 7)]
+SCALAR_CHUNK = 5
 STORE_FROM = {1: 0, 3: 2, 4: 4, 5: 5, 6: 6}
 PROJECT_LAG = 3
 DRAIN_LAG = 5
@@ -41,153 +46,145 @@ def tile_picked_lora_gelu_p_kernel(tc, x_words, x_scales, w1_words, w1_scales, w
         stage = ctx.enter_context(tc.tile_pool(name="stage", bufs=1))
         psum = ctx.enter_context(tc.psum_pool(name="psum", bufs=1))
 
-        offsets = keep.tile([P, S // 16], U16, name="offsets")
-        xs = keep.tile([P, T], U8, name="xs", tag="scale_rows", align_bytes=64)
-        xw = keep.tile([P, T], U32, name="xw", align_bytes=64)
-        raw = [stage.tile([P, PACK, HALF], F32, name=f"raw{a}", offset=a * PACK * HALF * 4, align_bytes=64) for a in range(2)]
-        w2b = keep.tile([P, PACK, P, PACK], BF16, name="w2b", align_bytes=64)
-        w2w = keep.tile([P, H], U32, name="w2w", align_bytes=64)
-        w2s = keep.tile([P, H], U8, name="w2s", align_bytes=64)
-        warm = keep.tile([P, 2], F32, name="warm", align_bytes=64)
-        early_plane = keep.tile([P, S // 2], U8, name="early_plane", align_bytes=64)
-        late_planes = keep.tile([P, S // 2 + 2 * N], U8, name="late_planes", align_bytes=64)
-        w1s = late_planes[:, S // 2 : S // 2 + N]
-        w3s = late_planes[:, S // 2 + N : S // 2 + 2 * N]
-        picked = [keep.tile([P, S // 2], U8, name=f"picked{a}", align_bytes=64) for a in range(2)]
-        gw = [keep.tile([P, GATHER], U32, name=f"gw{g}", align_bytes=64) for g in range(S // GATHER)]
+        offsets = keep.tile([P, S // LIST_ROWS], U16, name="offsets")
+        scale_window = keep.tile([P, T], U8, name="scale_window", tag="scale_window", align_bytes=64)
+        word_window = keep.tile([P, T], U32, name="word_window", align_bytes=64)
+        w2_raw = [stage.tile([P, PACK, HALF_H], F32, name=f"w2_raw{a}", offset=a * PACK * HALF_H * 4, align_bytes=64) for a in range(2)]
+        w2_bf16 = keep.tile([P, PACK, P, PACK], BF16, name="w2_bf16", align_bytes=64)
+        w2_words = keep.tile([P, H], U32, name="w2_words", align_bytes=64)
+        w2_plane = keep.tile([P, H], U8, name="w2_plane", align_bytes=64)
+        preload = keep.tile([P, 2], F32, name="preload", align_bytes=64)
+        early_plane = keep.tile([P, HALF_TOKENS], U8, name="early_plane", align_bytes=64)
+        late_planes = keep.tile([P, HALF_TOKENS + 2 * N], U8, name="late_planes", align_bytes=64)
+        w1_cols = slice(HALF_TOKENS, HALF_TOKENS + N)
+        w3_cols = slice(HALF_TOKENS + N, HALF_TOKENS + 2 * N)
+        w1_plane = late_planes[:, w1_cols]
+        w3_plane = late_planes[:, w3_cols]
+        x_planes = [early_plane, late_planes]
+        picked_rows = [keep.tile([P, HALF_TOKENS], U8, name=f"picked_rows{a}", align_bytes=64) for a in range(2)]
+        x_codes = [keep.tile([P, GATHER], U32, name=f"x_codes{g}", align_bytes=64) for g in range(S // GATHER)]
 
-        nc.vector.memset(warm[:, 0:1], 0.0)
-        for rows in (slice(0, 16), slice(32, 64), slice(64, P)):
-            nc.vector.memset(xs[rows, :].bitcast(I32), 0)
+        nc.vector.memset(preload[:, 0:1], 0.0)
+        for rows in (slice(0, STAGED.start), slice(STAGED.stop, 64), slice(64, P)):
+            nc.vector.memset(scale_window[rows, :].bitcast(I32), 0)
         nc.vector.memset(early_plane[:].bitcast(I32), 0)
         nc.vector.memset(late_planes[:].bitcast(I32), 0)
-        nc.scalar.activation(out=warm[:, 1:2], in_=warm[:, 0:1], func=GELU)
+        nc.scalar.dma_start(out=scale_window[STAGED, :].bitcast(I32), in_=x_scales[0].bitcast(I32))
+        nc.scalar.activation(out=preload[:, 1:2], in_=preload[:, 0:1], func=GELU)
 
-        w2v = w2.rearrange("(p j) c -> p j c", j=PACK)
+        w2_rows = w2.rearrange("(p j) c -> p j c", j=PACK)
         nc.sync.dma_start(offsets[:], offs)
-        nc.sync.dma_start(out=xs[16:32, :].bitcast(I32), in_=x_scales[0].bitcast(I32))
         for a in range(2):
-            nc.sync.dma_start(out=raw[a][:], in_=w2v[:, :, a * HALF : (a + 1) * HALF])
-        nc.sync.dma_start(out=xw[:].bitcast(I32), in_=words_of(x_words))
+            nc.sync.dma_start(out=w2_raw[a][:], in_=w2_rows[:, :, a * HALF_H : (a + 1) * HALF_H])
+        nc.sync.dma_start(out=word_window[:].bitcast(I32), in_=words_of(x_words))
 
         def place_scales(queue, plane, rows):
             for r in range(4):
-                queue.dma_start(out=plane[r:P:32, :].bitcast(I32), in_=rows[16 + r : 32 : 4, :].bitcast(I32))
+                queue.dma_start(out=plane[r:P:32, :].bitcast(I32), in_=rows[STAGED.start + r : STAGED.stop : 4, :].bitcast(I32))
 
         for a in range(2):
-            nc.vector.tensor_copy(picked[a][:], xs[:].indirect(offsets[:, a * S // 32 : (a + 1) * S // 32]))
-        ww = keep.tile([P, 2 * N], U32, name="ww", tag="scale_rows", align_bytes=64)
-        w1w = ww[:, 0:N]
-        w3w = ww[:, N : 2 * N]
-        place_scales(nc.sync, early_plane, picked[0])
-        nc.sync.dma_start(out=w1w.bitcast(I32), in_=words_of(w1_words))
-        nc.sync.dma_start(out=w3w.bitcast(I32), in_=words_of(w3_words))
+            entries = slice(a * HALF_TOKENS // LIST_ROWS, (a + 1) * HALF_TOKENS // LIST_ROWS)
+            nc.vector.tensor_copy(picked_rows[a][:], scale_window[:].indirect(offsets[:, entries]))
+        w_words = keep.tile([P, 2 * N], U32, name="w_words", tag="scale_window", align_bytes=64)
+        w1_codes = w_words[:, 0:N]
+        w3_codes = w_words[:, N : 2 * N]
+        place_scales(nc.sync, early_plane, picked_rows[0])
+        nc.sync.dma_start(out=w1_codes.bitcast(I32), in_=words_of(w1_words))
+        nc.sync.dma_start(out=w3_codes.bitcast(I32), in_=words_of(w3_words))
 
-        def regroup(copy, a, m0, m1):
+        def regroup(copy, a, first, last):
             copy(
-                out=w2b[:, :, 64 * a + m0 : 64 * a + m1, :].rearrange("p t m j -> p m j t"),
-                in_=raw[a][:, :, PACK * m0 : PACK * m1].rearrange("p j (m t) -> p m j t", t=PACK),
+                out=w2_bf16[:, :, GROUPS * a + first : GROUPS * a + last, :].rearrange("p t m j -> p m j t"),
+                in_=w2_raw[a][:, :, PACK * first : PACK * last].rearrange("p j (m t) -> p m j t", t=PACK),
             )
 
-        regroup(nc.scalar.copy, 0, 0, 64)
-        late_rows = stage.tile([P, S // 2 + 2 * N], U8, name="late_rows", offset=0, align_bytes=64)
-        nc.scalar.dma_start(out=late_rows[16:32, S // 2 : S // 2 + N].bitcast(I32), in_=w1_scales[0].bitcast(I32))
-        nc.scalar.dma_start(out=late_rows[16:32, S // 2 + N : S // 2 + 2 * N].bitcast(I32), in_=w3_scales[0].bitcast(I32))
-        regroup(nc.scalar.copy, 1, 0, SCALAR_SHARE)
-        nc.vector.tensor_copy(out=late_rows[:, 0 : S // 2].bitcast(I32), in_=picked[1][:].bitcast(I32))
-        regroup(nc.vector.tensor_copy, 1, SCALAR_SHARE, 64)
+        regroup(nc.scalar.copy, 0, 0, GROUPS)
+        late_rows = stage.tile([P, HALF_TOKENS + 2 * N], U8, name="late_rows", offset=0, align_bytes=64)
+        nc.scalar.dma_start(out=late_rows[STAGED, w1_cols].bitcast(I32), in_=w1_scales[0].bitcast(I32))
+        nc.scalar.dma_start(out=late_rows[STAGED, w3_cols].bitcast(I32), in_=w3_scales[0].bitcast(I32))
+        regroup(nc.scalar.copy, 1, 0, SCALAR_GROUPS)
+        nc.vector.tensor_copy(out=late_rows[:, 0:HALF_TOKENS].bitcast(I32), in_=picked_rows[1][:].bitcast(I32))
+        regroup(nc.vector.tensor_copy, 1, SCALAR_GROUPS, GROUPS)
         place_scales(nc.scalar, late_planes, late_rows)
-        gs = [early_plane, late_planes]
         for t in range(PACK):
             cols = slice(t * P, (t + 1) * P)
-            nc.vector.quantize_mx(out=w2w[:, cols].bitcast(FP8X4), scales=w2s[:, cols], in_=w2b[:, t].rearrange("p m j -> p (m j)"))
+            nc.vector.quantize_mx(out=w2_words[:, cols].bitcast(FP8X4), scales=w2_plane[:, cols], in_=w2_bf16[:, t].rearrange("p m j -> p (m j)"))
         scrap = psum.tile([P, 4 * P], F32, name="scrap", tag="bank7")
         for width in WARM_UP:
-            nc.tensor.matmul_mx(out=scrap[:, 0:width], lhsT=w2w[:, 0:P].bitcast(FP8X4), lhsT_scale=w2s[:, 0:P], rhs=w2w[:, 0:width].bitcast(FP8X4), rhs_scale=w2s[:, 0:width], start=True, stop=True)
+            nc.tensor.matmul_mx(out=scrap[:, 0:width], lhsT=w2_words[:, 0:P].bitcast(FP8X4), lhsT_scale=w2_plane[:, 0:P], rhs=w2_words[:, 0:width].bitcast(FP8X4), rhs_scale=w2_plane[:, 0:width], start=True, stop=True)
         for g in range(S // GATHER):
-            cols = slice(g * GATHER // 16, (g + 1) * GATHER // 16)
-            nc.vector.tensor_copy(gw[g][:], xw[:].indirect(offsets[:, cols]))
+            entries = slice(g * GATHER // LIST_ROWS, (g + 1) * GATHER // LIST_ROWS)
+            nc.vector.tensor_copy(x_codes[g][:], word_window[:].indirect(offsets[:, entries]))
 
-        outv = out.rearrange("(m p) n -> p m n", p=P)
-        hw = keep.tile([P, S], U32, name="hw", align_bytes=64)
-        hs = keep.tile([P, S], U8, name="hs", align_bytes=64)
+        out_halves = out.rearrange("(m p) n -> p m n", p=P)
+        h_words = keep.tile([P, S], U32, name="h_words", align_bytes=64)
+        h_plane = keep.tile([P, S], U8, name="h_plane", align_bytes=64)
+        results = keep.tile([P, 2, S - CHUNK], F32, name="results", align_bytes=64)
 
-        def x_operand(n0):
-            g, o = divmod(n0, GATHER)
-            return gw[g][:, o : o + CHUNK].bitcast(FP8X4), gs[n0 // (S // 2)][:, n0 % (S // 2) : n0 % (S // 2) + CHUNK]
+        def tokens(c):
+            return slice(c * CHUNK, (c + 1) * CHUNK)
+
+        def x_operand(c):
+            g, word_at = divmod(c * CHUNK, GATHER)
+            half, byte_at = divmod(c * CHUNK, HALF_TOKENS)
+            return x_codes[g][:, word_at : word_at + CHUNK], x_planes[half][:, byte_at : byte_at + CHUNK]
+
+        def product(dst, codes, plane, block, moving_codes, moving_plane, start, stop):
+            cols = slice(block * P, (block + 1) * P)
+            nc.tensor.matmul_mx(out=dst, lhsT=codes[:, cols].bitcast(FP8X4), lhsT_scale=plane[:, cols], rhs=moving_codes.bitcast(FP8X4), rhs_scale=moving_plane, start=start, stop=stop)
 
         def hidden(c):
-            hp = psum.tile([P, PACK, CHUNK], F32, name="hp", tag=f"bank{c % 4}")
-            xq, xsc = x_operand(c * CHUNK)
+            bank = psum.tile([P, PACK, CHUNK], F32, name="h_sums", tag=f"bank{c % H_BANKS}")
             for t in range(PACK):
-                cols = slice(t * P, (t + 1) * P)
-                nc.tensor.matmul_mx(out=hp[:, t, :], lhsT=w2w[:, cols].bitcast(FP8X4), lhsT_scale=w2s[:, cols], rhs=xq, rhs_scale=xsc, start=True, stop=True)
-            return hp
+                product(bank[:, t, :], w2_words, w2_plane, t, *x_operand(c), True, True)
+            h_bf16 = keep.tile([P, CHUNK, PACK], BF16, name=f"h_bf16_{c}", align_bytes=64)
+            nc.scalar.activation(out=h_bf16[:], in_=bank[:].rearrange("p t n -> p n t"), func=GELU)
+            return h_bf16
 
-        def activate(hp, a, b):
-            hb = keep.tile([P, b - a, PACK], BF16, name=f"hb{len(staged)}", align_bytes=64)
-            nc.scalar.activation(out=hb[:], in_=hp[:, :, a:b].rearrange("p t n -> p n t"), func=GELU)
-            staged.append(hb)
-
-        def own_term(dst, m, n0):
-            cols = slice(m * P, (m + 1) * P)
-            xq, xsc = x_operand(n0)
-            nc.tensor.matmul_mx(out=dst, lhsT=w1w[:, cols].bitcast(FP8X4), lhsT_scale=w1s[:, cols], rhs=xq, rhs_scale=xsc, start=True, stop=False)
-
-        def adapter_term(dst, m, n0):
-            cols = slice(m * P, (m + 1) * P)
-            nc.tensor.matmul_mx(out=dst, lhsT=w3w[:, cols].bitcast(FP8X4), lhsT_scale=w3s[:, cols], rhs=hw[:, n0 : n0 + CHUNK].bitcast(FP8X4), rhs_scale=hs[:, n0 : n0 + CHUNK], start=False, stop=True)
-
-        def project(u):
-            first, last = PIECES[u]
-            n0 = last - CHUNK
-            banks = OUT_BANKS[u]
+        def project(c, h_bf16):
+            banks = OUT_BANKS[c]
+            h_operand = (h_words[:, tokens(c)], h_plane[:, tokens(c)])
             if len(banks) == 2:
-                accs = [psum.tile([P, CHUNK], F32, name=f"half{m}", tag=f"bank{banks[m]}") for m in range(2)]
+                halves = [psum.tile([P, CHUNK], F32, name=f"out_half{m}", tag=f"bank{banks[m]}") for m in range(2)]
                 for m in range(2):
-                    own_term(accs[m][:], m, n0)
-            nc.vector.quantize_mx(out=hw[:, first:last].bitcast(FP8X4), scales=hs[:, first:last], in_=staged[u][:].rearrange("p n t -> p (n t)"))
+                    product(halves[m][:], w1_codes, w1_plane, m, *x_operand(c), True, False)
+            nc.vector.quantize_mx(out=h_operand[0].bitcast(FP8X4), scales=h_operand[1], in_=h_bf16[:].rearrange("p n t -> p (n t)"))
             if len(banks) == 2:
                 for m in range(2):
-                    adapter_term(accs[m][:], m, n0)
-                return accs
-            acc = psum.tile([P, 2, CHUNK], F32, name="acc", tag=f"bank{banks[0]}")
+                    product(halves[m][:], w3_codes, w3_plane, m, *h_operand, False, True)
+                return halves
+            both = psum.tile([P, 2, CHUNK], F32, name="out_both", tag=f"bank{banks[0]}")
             for m in range(2):
-                own_term(acc[:, m, :], m, n0)
-                adapter_term(acc[:, m, :], m, n0)
-            return acc
+                product(both[:, m, :], w1_codes, w1_plane, m, *x_operand(c), True, False)
+                product(both[:, m, :], w3_codes, w3_plane, m, *h_operand, False, True)
+            return both
 
-        def drain(u, acc):
-            first, last = PIECES[u]
-            if u == len(PIECES) - 1:
-                res = [keep.tile([P, CHUNK], F32, name=f"last_res{m}", align_bytes=64) for m in range(2)]
-                nc.scalar.copy(out=res[0][:], in_=acc[0][:])
-                nc.vector.tensor_copy(out=res[1][:], in_=acc[1][:])
-                nc.scalar.dma_start(out=out[0:P, first:last], in_=res[0][:])
-                nc.sync.dma_start(out=out[P : 2 * P, first:last], in_=res[1][:])
+        def drain(c, sums):
+            if c == CHUNKS - 1:
+                last = [keep.tile([P, CHUNK], F32, name=f"last{m}", align_bytes=64) for m in range(2)]
+                nc.scalar.copy(out=last[0][:], in_=sums[0][:])
+                nc.vector.tensor_copy(out=last[1][:], in_=sums[1][:])
+                nc.scalar.dma_start(out=out[0:P, tokens(c)], in_=last[0][:])
+                nc.sync.dma_start(out=out[P : 2 * P, tokens(c)], in_=last[1][:])
                 return
-            res = results[:, :, first:last]
-            if len(OUT_BANKS[u]) == 2:
-                nc.scalar.copy(out=res[:, 0, :], in_=acc[0][:])
-                nc.vector.tensor_copy(out=res[:, 1, :], in_=acc[1][:])
-            elif u in SCALAR_DRAINS:
-                nc.scalar.copy(out=res, in_=acc[:])
+            result = results[:, :, tokens(c)]
+            if len(OUT_BANKS[c]) == 2:
+                nc.scalar.copy(out=result[:, 0, :], in_=sums[0][:])
+                nc.vector.tensor_copy(out=result[:, 1, :], in_=sums[1][:])
+            elif c == SCALAR_CHUNK:
+                nc.scalar.copy(out=result, in_=sums[:])
             else:
-                nc.vector.tensor_copy(out=res, in_=acc[:])
-            if u in STORE_FROM:
-                cols = slice(STORE_FROM[u] * CHUNK, last)
-                nc.sync.dma_start(out=outv[:, :, cols], in_=results[:, :, cols])
+                nc.vector.tensor_copy(out=result, in_=sums[:])
+            if c in STORE_FROM:
+                cols = slice(STORE_FROM[c] * CHUNK, (c + 1) * CHUNK)
+                nc.sync.dma_start(out=out_halves[:, :, cols], in_=results[:, :, cols])
 
-        results = keep.tile([P, 2, S - CHUNK], F32, name="results", align_bytes=64)
-        staged = []
-        sums = []
-        for step in range(len(PIECES) + DRAIN_LAG):
+        activated = []
+        summed = []
+        for step in range(CHUNKS + DRAIN_LAG):
             if step < CHUNKS:
-                hp = hidden(step)
-                for first, last in PIECES:
-                    if first // CHUNK == step:
-                        activate(hp, first - step * CHUNK, last - step * CHUNK)
-            if 0 <= step - PROJECT_LAG < len(PIECES):
-                sums.append(project(step - PROJECT_LAG))
+                activated.append(hidden(step))
+            if 0 <= step - PROJECT_LAG < CHUNKS:
+                summed.append(project(step - PROJECT_LAG, activated[step - PROJECT_LAG]))
             if step >= DRAIN_LAG:
-                drain(step - DRAIN_LAG, sums[step - DRAIN_LAG])
+                drain(step - DRAIN_LAG, summed[step - DRAIN_LAG])

@@ -19,14 +19,15 @@ PACK = 4
 LIST_ROWS = 16
 BLOCKS = 16
 STAGED = slice(16, 16 + BLOCKS)
-GATHER = 256
+GATHERS = [128, 128, 256, 256, 256]
+GATHER_AT = [sum(GATHERS[:g]) for g in range(len(GATHERS))]
 CHUNK = 128
 CHUNKS = S // CHUNK
 HALF_TOKENS = S // 2
 HALF_H = H // 2
 GROUPS = HALF_H // PACK
 SCALAR_GROUPS = 26
-WARM_UP = [128, 256, 256, 256, 256]
+WARM_UP = [256, 256, 256]
 H_BANKS = 4
 OUT_BANKS = [(4,), (5,), (6,), (7,), (4,), (5,), (6, 0), (1, 7)]
 SCALAR_CHUNK = 5
@@ -62,7 +63,7 @@ def tile_picked_lora_gelu_p_kernel(tc, x_words, x_scales, w1_words, w1_scales, w
         w3_plane = late_planes[:, w3_cols]
         x_planes = [early_plane, late_planes]
         picked_rows = [keep.tile([P, HALF_TOKENS], U8, name=f"picked_rows{a}", align_bytes=64) for a in range(2)]
-        x_codes = [keep.tile([P, GATHER], U32, name=f"x_codes{g}", align_bytes=64) for g in range(S // GATHER)]
+        x_codes = [keep.tile([P, width], U32, name=f"x_codes{g}", align_bytes=64) for g, width in enumerate(GATHERS)]
 
         nc.vector.memset(preload[:, 0:1], 0.0)
         for rows in (slice(0, STAGED.start), slice(STAGED.stop, 64), slice(64, P)):
@@ -112,8 +113,8 @@ def tile_picked_lora_gelu_p_kernel(tc, x_words, x_scales, w1_words, w1_scales, w
         scrap = psum.tile([P, 4 * P], F32, name="scrap", tag="bank7")
         for width in WARM_UP:
             nc.tensor.matmul_mx(out=scrap[:, 0:width], lhsT=w2_words[:, 0:P].bitcast(FP8X4), lhsT_scale=w2_plane[:, 0:P], rhs=w2_words[:, 0:width].bitcast(FP8X4), rhs_scale=w2_plane[:, 0:width], start=True, stop=True)
-        for g in range(S // GATHER):
-            entries = slice(g * GATHER // LIST_ROWS, (g + 1) * GATHER // LIST_ROWS)
+        for g, width in enumerate(GATHERS):
+            entries = slice(GATHER_AT[g] // LIST_ROWS, (GATHER_AT[g] + width) // LIST_ROWS)
             nc.vector.tensor_copy(x_codes[g][:], word_window[:].indirect(offsets[:, entries]))
 
         out_halves = out.rearrange("(m p) n -> p m n", p=P)
@@ -125,7 +126,8 @@ def tile_picked_lora_gelu_p_kernel(tc, x_words, x_scales, w1_words, w1_scales, w
             return slice(c * CHUNK, (c + 1) * CHUNK)
 
         def x_operand(c):
-            g, word_at = divmod(c * CHUNK, GATHER)
+            g = max(n for n, at in enumerate(GATHER_AT) if at <= c * CHUNK)
+            word_at = c * CHUNK - GATHER_AT[g]
             half, byte_at = divmod(c * CHUNK, HALF_TOKENS)
             return x_codes[g][:, word_at : word_at + CHUNK], x_planes[half][:, byte_at : byte_at + CHUNK]
 

@@ -18,7 +18,7 @@ P = 128
 PACK = 4
 LIST_ROWS = 16
 BLOCKS = 16
-STAGED = slice(16, 16 + BLOCKS)
+STAGED = slice(32, 32 + 4 * BLOCKS, 4)
 GATHERS = [128, 128, 256, 256, 256]
 GATHER_AT = [sum(GATHERS[:g]) for g in range(len(GATHERS))]
 CHUNK = 128
@@ -65,9 +65,8 @@ def tile_picked_lora_gelu_p_kernel(tc, x_words, x_scales, w1_words, w1_scales, w
         picked_rows = [keep.tile([P, HALF_TOKENS], U8, name=f"picked_rows{a}", align_bytes=64) for a in range(2)]
         x_codes = [keep.tile([P, width], U32, name=f"x_codes{g}", align_bytes=64) for g, width in enumerate(GATHERS)]
 
+        nc.vector.memset(scale_window[:].bitcast(I32), 0)
         nc.vector.memset(preload[:, 0:1], 0.0)
-        for rows in (slice(0, STAGED.start), slice(STAGED.stop, 64), slice(64, P)):
-            nc.vector.memset(scale_window[rows, :].bitcast(I32), 0)
         nc.vector.memset(early_plane[:].bitcast(I32), 0)
         nc.vector.memset(late_planes[:].bitcast(I32), 0)
         nc.scalar.dma_start(out=scale_window[STAGED, :].bitcast(I32), in_=x_scales[0].bitcast(I32))
@@ -81,7 +80,7 @@ def tile_picked_lora_gelu_p_kernel(tc, x_words, x_scales, w1_words, w1_scales, w
 
         def place_scales(queue, plane, rows):
             for r in range(4):
-                queue.dma_start(out=plane[r:P:32, :].bitcast(I32), in_=rows[STAGED.start + r : STAGED.stop : 4, :].bitcast(I32))
+                queue.dma_start(out=plane[r:P:32, :].bitcast(I32), in_=rows[STAGED.start + 4 * r : STAGED.stop : 16, :].bitcast(I32))
 
         for a in range(2):
             entries = slice(a * HALF_TOKENS // LIST_ROWS, (a + 1) * HALF_TOKENS // LIST_ROWS)
@@ -90,8 +89,6 @@ def tile_picked_lora_gelu_p_kernel(tc, x_words, x_scales, w1_words, w1_scales, w
         w1_codes = w_words[:, 0:N]
         w3_codes = w_words[:, N : 2 * N]
         place_scales(nc.sync, early_plane, picked_rows[0])
-        nc.sync.dma_start(out=w1_codes.bitcast(I32), in_=words_of(w1_words))
-        nc.sync.dma_start(out=w3_codes.bitcast(I32), in_=words_of(w3_words))
 
         def regroup(copy, a, first, last):
             copy(
@@ -101,12 +98,14 @@ def tile_picked_lora_gelu_p_kernel(tc, x_words, x_scales, w1_words, w1_scales, w
 
         regroup(nc.scalar.copy, 0, 0, GROUPS)
         late_rows = stage.tile([P, HALF_TOKENS + 2 * N], U8, name="late_rows", offset=0, align_bytes=64)
-        nc.scalar.dma_start(out=late_rows[STAGED, w1_cols].bitcast(I32), in_=w1_scales[0].bitcast(I32))
-        nc.scalar.dma_start(out=late_rows[STAGED, w3_cols].bitcast(I32), in_=w3_scales[0].bitcast(I32))
+        nc.sync.dma_start(out=late_rows[STAGED, w1_cols].bitcast(I32), in_=w1_scales[0].bitcast(I32))
+        nc.sync.dma_start(out=late_rows[STAGED, w3_cols].bitcast(I32), in_=w3_scales[0].bitcast(I32))
+        nc.sync.dma_start(out=w1_codes.bitcast(I32), in_=words_of(w1_words))
+        nc.sync.dma_start(out=w3_codes.bitcast(I32), in_=words_of(w3_words))
         regroup(nc.scalar.copy, 1, 0, SCALAR_GROUPS)
         nc.vector.tensor_copy(out=late_rows[:, 0:HALF_TOKENS].bitcast(I32), in_=picked_rows[1][:].bitcast(I32))
         regroup(nc.vector.tensor_copy, 1, SCALAR_GROUPS, GROUPS)
-        place_scales(nc.scalar, late_planes, late_rows)
+        place_scales(nc.sync, late_planes, late_rows)
         for t in range(PACK):
             cols = slice(t * P, (t + 1) * P)
             nc.vector.quantize_mx(out=w2_words[:, cols].bitcast(FP8X4), scales=w2_plane[:, cols], in_=w2_bf16[:, t].rearrange("p m j -> p (m j)"))

@@ -18,22 +18,21 @@ P = 128
 PACK = 4
 LIST_ROWS = 16
 BLOCKS = 16
-STAGED = slice(32, 32 + 4 * BLOCKS, 4)
+STAGED = slice(16, 16 + BLOCKS)
 GATHERS = [128, 128, 256, 256, 256]
 GATHER_AT = [sum(GATHERS[:g]) for g in range(len(GATHERS))]
 CHUNK = 128
 CHUNKS = S // CHUNK
-HALF_TOKENS = S // 2
 HALF_H = H // 2
 GROUPS = HALF_H // PACK
 SCALAR_GROUPS = 26
 WARM_UP = [256, 256, 256]
-H_BANKS = 4
-OUT_BANKS = [(4,), (5,), (6,), (7,), (4,), (5,), (6, 0), (1, 7)]
+H_BANKS = [0, 1, 2, 3, 0, 2, 3, 0]
+H_AHEAD = 5
+OUT_BANKS = [(4,), (5,), (6,), (7,), (1,), (4,), (5, 2), (6, 3)]
 SCALAR_CHUNK = 5
 STORE_FROM = {1: 0, 3: 2, 4: 4, 5: 5, 6: 6}
-PROJECT_LAG = 3
-DRAIN_LAG = 5
+DRAIN_LAG = 2
 
 
 def words_of(dram):
@@ -55,20 +54,21 @@ def tile_picked_lora_gelu_p_kernel(tc, x_words, x_scales, w1_words, w1_scales, w
         w2_words = keep.tile([P, H], U32, name="w2_words", align_bytes=64)
         w2_plane = keep.tile([P, H], U8, name="w2_plane", align_bytes=64)
         preload = keep.tile([P, 2], F32, name="preload", align_bytes=64)
-        early_plane = keep.tile([P, HALF_TOKENS], U8, name="early_plane", align_bytes=64)
-        late_planes = keep.tile([P, HALF_TOKENS + 2 * N], U8, name="late_planes", align_bytes=64)
-        w1_cols = slice(HALF_TOKENS, HALF_TOKENS + N)
-        w3_cols = slice(HALF_TOKENS + N, HALF_TOKENS + 2 * N)
-        w1_plane = late_planes[:, w1_cols]
-        w3_plane = late_planes[:, w3_cols]
-        x_planes = [early_plane, late_planes]
-        picked_rows = [keep.tile([P, HALF_TOKENS], U8, name=f"picked_rows{a}", align_bytes=64) for a in range(2)]
+        x_plane = keep.tile([P, S], U8, name="x_plane", align_bytes=64)
+        w_planes = keep.tile([P, 2 * N], U8, name="w_planes", align_bytes=64)
+        w_rows = keep.tile([P, 2 * N], U8, name="w_rows", align_bytes=64)
+        w1_cols = slice(0, N)
+        w3_cols = slice(N, 2 * N)
+        w1_plane = w_planes[:, w1_cols]
+        w3_plane = w_planes[:, w3_cols]
+        picked_rows = keep.tile([P, S], U8, name="picked_rows", align_bytes=64)
         x_codes = [keep.tile([P, width], U32, name=f"x_codes{g}", align_bytes=64) for g, width in enumerate(GATHERS)]
 
-        nc.vector.memset(scale_window[:].bitcast(I32), 0)
+        for rows in (slice(0, STAGED.start), slice(STAGED.stop, 64), slice(64, P)):
+            nc.vector.memset(scale_window[rows, :].bitcast(I32), 0)
         nc.vector.memset(preload[:, 0:1], 0.0)
-        nc.vector.memset(early_plane[:].bitcast(I32), 0)
-        nc.vector.memset(late_planes[:].bitcast(I32), 0)
+        nc.vector.memset(x_plane[:].bitcast(I32), 0)
+        nc.vector.memset(w_planes[:].bitcast(I32), 0)
         nc.scalar.dma_start(out=scale_window[STAGED, :].bitcast(I32), in_=x_scales[0].bitcast(I32))
         nc.scalar.activation(out=preload[:, 1:2], in_=preload[:, 0:1], func=GELU)
 
@@ -77,18 +77,20 @@ def tile_picked_lora_gelu_p_kernel(tc, x_words, x_scales, w1_words, w1_scales, w
         for a in range(2):
             nc.sync.dma_start(out=w2_raw[a][:], in_=w2_rows[:, :, a * HALF_H : (a + 1) * HALF_H])
         nc.sync.dma_start(out=word_window[:].bitcast(I32), in_=words_of(x_words))
+        nc.sync.dma_start(out=w_rows[STAGED, w1_cols].bitcast(I32), in_=w1_scales[0].bitcast(I32))
+        nc.sync.dma_start(out=w_rows[STAGED, w3_cols].bitcast(I32), in_=w3_scales[0].bitcast(I32))
 
         def place_scales(queue, plane, rows):
             for r in range(4):
-                queue.dma_start(out=plane[r:P:32, :].bitcast(I32), in_=rows[STAGED.start + 4 * r : STAGED.stop : 16, :].bitcast(I32))
+                queue.dma_start(out=plane[r:P:32, :].bitcast(I32), in_=rows[STAGED.start + r : STAGED.stop : 4, :].bitcast(I32))
 
-        for a in range(2):
-            entries = slice(a * HALF_TOKENS // LIST_ROWS, (a + 1) * HALF_TOKENS // LIST_ROWS)
-            nc.vector.tensor_copy(picked_rows[a][:], scale_window[:].indirect(offsets[:, entries]))
+        nc.vector.tensor_copy(picked_rows[:], scale_window[:].indirect(offsets[:]))
         w_words = keep.tile([P, 2 * N], U32, name="w_words", tag="scale_window", align_bytes=64)
         w1_codes = w_words[:, 0:N]
         w3_codes = w_words[:, N : 2 * N]
-        place_scales(nc.sync, early_plane, picked_rows[0])
+        place_scales(nc.sync, x_plane, picked_rows)
+        nc.sync.dma_start(out=w1_codes.bitcast(I32), in_=words_of(w1_words))
+        nc.sync.dma_start(out=w3_codes.bitcast(I32), in_=words_of(w3_words))
 
         def regroup(copy, a, first, last):
             copy(
@@ -97,15 +99,9 @@ def tile_picked_lora_gelu_p_kernel(tc, x_words, x_scales, w1_words, w1_scales, w
             )
 
         regroup(nc.scalar.copy, 0, 0, GROUPS)
-        late_rows = stage.tile([P, HALF_TOKENS + 2 * N], U8, name="late_rows", offset=0, align_bytes=64)
-        nc.sync.dma_start(out=late_rows[STAGED, w1_cols].bitcast(I32), in_=w1_scales[0].bitcast(I32))
-        nc.sync.dma_start(out=late_rows[STAGED, w3_cols].bitcast(I32), in_=w3_scales[0].bitcast(I32))
-        nc.sync.dma_start(out=w1_codes.bitcast(I32), in_=words_of(w1_words))
-        nc.sync.dma_start(out=w3_codes.bitcast(I32), in_=words_of(w3_words))
         regroup(nc.scalar.copy, 1, 0, SCALAR_GROUPS)
-        nc.vector.tensor_copy(out=late_rows[:, 0:HALF_TOKENS].bitcast(I32), in_=picked_rows[1][:].bitcast(I32))
         regroup(nc.vector.tensor_copy, 1, SCALAR_GROUPS, GROUPS)
-        place_scales(nc.sync, late_planes, late_rows)
+        place_scales(nc.scalar, w_planes, w_rows)
         for t in range(PACK):
             cols = slice(t * P, (t + 1) * P)
             nc.vector.quantize_mx(out=w2_words[:, cols].bitcast(FP8X4), scales=w2_plane[:, cols], in_=w2_bf16[:, t].rearrange("p m j -> p (m j)"))
@@ -127,38 +123,37 @@ def tile_picked_lora_gelu_p_kernel(tc, x_words, x_scales, w1_words, w1_scales, w
         def x_operand(c):
             g = max(n for n, at in enumerate(GATHER_AT) if at <= c * CHUNK)
             word_at = c * CHUNK - GATHER_AT[g]
-            half, byte_at = divmod(c * CHUNK, HALF_TOKENS)
-            return x_codes[g][:, word_at : word_at + CHUNK], x_planes[half][:, byte_at : byte_at + CHUNK]
+            return x_codes[g][:, word_at : word_at + CHUNK], x_plane[:, tokens(c)]
 
         def product(dst, codes, plane, block, moving_codes, moving_plane, start, stop):
             cols = slice(block * P, (block + 1) * P)
             nc.tensor.matmul_mx(out=dst, lhsT=codes[:, cols].bitcast(FP8X4), lhsT_scale=plane[:, cols], rhs=moving_codes.bitcast(FP8X4), rhs_scale=moving_plane, start=start, stop=stop)
 
         def hidden(c):
-            bank = psum.tile([P, PACK, CHUNK], F32, name="h_sums", tag=f"bank{c % H_BANKS}")
+            bank = psum.tile([P, PACK, CHUNK], F32, name="h_sums", tag=f"bank{H_BANKS[c]}")
             for t in range(PACK):
                 product(bank[:, t, :], w2_words, w2_plane, t, *x_operand(c), True, True)
             h_bf16 = keep.tile([P, CHUNK, PACK], BF16, name=f"h_bf16_{c}", align_bytes=64)
             nc.scalar.activation(out=h_bf16[:], in_=bank[:].rearrange("p t n -> p n t"), func=GELU)
             return h_bf16
 
-        def project(c, h_bf16):
+        def open_sums(c):
             banks = OUT_BANKS[c]
-            h_operand = (h_words[:, tokens(c)], h_plane[:, tokens(c)])
             if len(banks) == 2:
-                halves = [psum.tile([P, CHUNK], F32, name=f"out_half{m}", tag=f"bank{banks[m]}") for m in range(2)]
-                for m in range(2):
-                    product(halves[m][:], w1_codes, w1_plane, m, *x_operand(c), True, False)
-            nc.vector.quantize_mx(out=h_operand[0].bitcast(FP8X4), scales=h_operand[1], in_=h_bf16[:].rearrange("p n t -> p (n t)"))
-            if len(banks) == 2:
-                for m in range(2):
-                    product(halves[m][:], w3_codes, w3_plane, m, *h_operand, False, True)
-                return halves
-            both = psum.tile([P, 2, CHUNK], F32, name="out_both", tag=f"bank{banks[0]}")
+                tiles = [psum.tile([P, CHUNK], F32, name=f"out_half{m}", tag=f"bank{banks[m]}") for m in range(2)]
+                halves = [tile[:] for tile in tiles]
+            else:
+                tiles = psum.tile([P, 2, CHUNK], F32, name="out_both", tag=f"bank{banks[0]}")
+                halves = [tiles[:, m, :] for m in range(2)]
             for m in range(2):
-                product(both[:, m, :], w1_codes, w1_plane, m, *x_operand(c), True, False)
-                product(both[:, m, :], w3_codes, w3_plane, m, *h_operand, False, True)
-            return both
+                product(halves[m], w1_codes, w1_plane, m, *x_operand(c), len(banks) == 2 or m == 0, False)
+            return tiles, halves
+
+        def close_sums(c, h_bf16, halves):
+            h_operand = (h_words[:, tokens(c)], h_plane[:, tokens(c)])
+            nc.vector.quantize_mx(out=h_operand[0].bitcast(FP8X4), scales=h_operand[1], in_=h_bf16[:].rearrange("p n t -> p (n t)"))
+            for m in range(2):
+                product(halves[m], w3_codes, w3_plane, m, *h_operand, False, len(OUT_BANKS[c]) == 2 or m == 1)
 
         def drain(c, sums):
             if c == CHUNKS - 1:
@@ -180,12 +175,14 @@ def tile_picked_lora_gelu_p_kernel(tc, x_words, x_scales, w1_words, w1_scales, w
                 cols = slice(STORE_FROM[c] * CHUNK, (c + 1) * CHUNK)
                 nc.sync.dma_start(out=out_halves[:, :, cols], in_=results[:, :, cols])
 
-        activated = []
+        activated = [hidden(c) for c in range(H_AHEAD)]
         summed = []
-        for step in range(CHUNKS + DRAIN_LAG):
-            if step < CHUNKS:
-                activated.append(hidden(step))
-            if 0 <= step - PROJECT_LAG < CHUNKS:
-                summed.append(project(step - PROJECT_LAG, activated[step - PROJECT_LAG]))
-            if step >= DRAIN_LAG:
-                drain(step - DRAIN_LAG, summed[step - DRAIN_LAG])
+        for c in range(CHUNKS + DRAIN_LAG):
+            if c < CHUNKS:
+                tiles, halves = open_sums(c)
+                close_sums(c, activated[c], halves)
+                summed.append(tiles)
+            if c >= DRAIN_LAG:
+                drain(c - DRAIN_LAG, summed[c - DRAIN_LAG])
+            if c >= 1 and len(activated) < CHUNKS:
+                activated.append(hidden(len(activated)))

@@ -33,6 +33,7 @@ OUT_BANKS = [(4,), (5,), (6,), (7,), (1,), (4,), (5, 2), (6, 3)]
 SCALAR_CHUNK = 5
 STORE_FROM = {1: 0, 3: 2, 4: 4, 5: 5, 6: 6}
 DRAIN_LAG = 2
+H_CODE_BUFFERS = [0, 1, 2, 3, 4, 3, 4, 5]
 
 
 def words_of(dram):
@@ -113,8 +114,6 @@ def tile_picked_lora_gelu_p_kernel(tc, x_words, x_scales, w1_words, w1_scales, w
             nc.vector.tensor_copy(x_codes[g][:], word_window[:].indirect(offsets[:, entries]))
 
         out_halves = out.rearrange("(m p) n -> p m n", p=P)
-        h_words = keep.tile([P, S], U32, name="h_words", align_bytes=64)
-        h_plane = keep.tile([P, S], U8, name="h_plane", align_bytes=64)
         results = keep.tile([P, 2, S - CHUNK], F32, name="results", align_bytes=64)
 
         def tokens(c):
@@ -150,7 +149,9 @@ def tile_picked_lora_gelu_p_kernel(tc, x_words, x_scales, w1_words, w1_scales, w
             return tiles, halves
 
         def close_sums(c, h_bf16, halves):
-            h_operand = (h_words[:, tokens(c)], h_plane[:, tokens(c)])
+            h_words = keep.tile([P, CHUNK], U32, name="h_words", tag=f"h_words{H_CODE_BUFFERS[c]}", align_bytes=64)
+            h_plane = keep.tile([P, CHUNK], U8, name="h_plane", tag=f"h_plane{H_CODE_BUFFERS[c]}", align_bytes=64)
+            h_operand = (h_words[:], h_plane[:])
             nc.vector.quantize_mx(out=h_operand[0].bitcast(FP8X4), scales=h_operand[1], in_=h_bf16[:].rearrange("p n t -> p (n t)"))
             for m in range(2):
                 product(halves[m], w3_codes, w3_plane, m, *h_operand, False, len(OUT_BANKS[c]) == 2 or m == 1)
@@ -178,11 +179,11 @@ def tile_picked_lora_gelu_p_kernel(tc, x_words, x_scales, w1_words, w1_scales, w
         activated = [hidden(c) for c in range(H_AHEAD)]
         summed = []
         for c in range(CHUNKS + DRAIN_LAG):
+            if c >= DRAIN_LAG:
+                drain(c - DRAIN_LAG, summed[c - DRAIN_LAG])
             if c < CHUNKS:
                 tiles, halves = open_sums(c)
                 close_sums(c, activated[c], halves)
                 summed.append(tiles)
-            if c >= DRAIN_LAG:
-                drain(c - DRAIN_LAG, summed[c - DRAIN_LAG])
             if c >= 1 and len(activated) < CHUNKS:
                 activated.append(hidden(len(activated)))

@@ -23,15 +23,16 @@ GATHERS = [128, 128, 256, 256, 256]
 GATHER_AT = [sum(GATHERS[:g]) for g in range(len(GATHERS))]
 CHUNK = 128
 CHUNKS = S // CHUNK
-HALF_H = H // 2
-GROUPS = HALF_H // PACK
-SCALAR_GROUPS = 26
-WARM_UP = [256, 256, 256]
+EARLY = 6 * CHUNK
+LATE = S - EARLY
+GROUPS = H // PACK
+SCALAR_GROUPS = 62
+WARM_UP = [128, 128, 256, 256]
 H_BANKS = [0, 1, 2, 3, 0, 2, 3, 0]
 H_AHEAD = 5
 OUT_BANKS = [(4,), (5,), (6,), (7,), (1,), (4,), (5, 2), (6, 3)]
 SCALAR_CHUNK = 5
-STORE_FROM = {1: 0, 3: 2, 4: 4, 5: 5, 6: 6}
+STORE_FROM = {1: 0, 3: 2, 4: 4, 5: 5}
 DRAIN_LAG = 2
 H_CODE_BUFFERS = [0, 1, 2, 3, 4, 3, 4, 5]
 
@@ -44,65 +45,66 @@ def tile_picked_lora_gelu_p_kernel(tc, x_words, x_scales, w1_words, w1_scales, w
     nc = tc.nc
     with ExitStack() as ctx:
         keep = ctx.enter_context(tc.tile_pool(name="keep", bufs=1))
-        stage = ctx.enter_context(tc.tile_pool(name="stage", bufs=1))
         psum = ctx.enter_context(tc.psum_pool(name="psum", bufs=1))
 
         offsets = keep.tile([P, S // LIST_ROWS], U16, name="offsets")
         scale_window = keep.tile([P, T], U8, name="scale_window", tag="scale_window", align_bytes=64)
         word_window = keep.tile([P, T], U32, name="word_window", align_bytes=64)
-        w2_raw = [stage.tile([P, PACK, HALF_H], F32, name=f"w2_raw{a}", offset=a * PACK * HALF_H * 4, align_bytes=64) for a in range(2)]
+        w2_raw = keep.tile([P, PACK, H], F32, name="w2_raw", align_bytes=64)
         w2_bf16 = keep.tile([P, PACK, P, PACK], BF16, name="w2_bf16", align_bytes=64)
         w2_words = keep.tile([P, H], U32, name="w2_words", align_bytes=64)
         w2_plane = keep.tile([P, H], U8, name="w2_plane", align_bytes=64)
         preload = keep.tile([P, 2], F32, name="preload", align_bytes=64)
-        x_plane = keep.tile([P, S], U8, name="x_plane", align_bytes=64)
-        w_planes = keep.tile([P, 2 * N], U8, name="w_planes", align_bytes=64)
-        w_rows = keep.tile([P, 2 * N], U8, name="w_rows", align_bytes=64)
-        w1_cols = slice(0, N)
-        w3_cols = slice(N, 2 * N)
-        w1_plane = w_planes[:, w1_cols]
-        w3_plane = w_planes[:, w3_cols]
-        picked_rows = keep.tile([P, S], U8, name="picked_rows", align_bytes=64)
+        early_plane = keep.tile([P, EARLY], U8, name="early_plane", align_bytes=64)
+        late_planes = keep.tile([P, LATE + 2 * N], U8, name="late_planes", align_bytes=64)
+        late_rows = keep.tile([P, LATE + 2 * N], U8, name="late_rows", align_bytes=64)
+        w1_cols = slice(LATE, LATE + N)
+        w3_cols = slice(LATE + N, LATE + 2 * N)
+        w1_plane = late_planes[:, w1_cols]
+        w3_plane = late_planes[:, w3_cols]
+        picked_early = keep.tile([P, EARLY], U8, name="picked_early", align_bytes=64)
+        picked_late = keep.tile([P, LATE], U8, name="picked_late", align_bytes=64)
         x_codes = [keep.tile([P, width], U32, name=f"x_codes{g}", align_bytes=64) for g, width in enumerate(GATHERS)]
 
         for rows in (slice(0, STAGED.start), slice(STAGED.stop, 64), slice(64, P)):
             nc.vector.memset(scale_window[rows, :].bitcast(I32), 0)
         nc.vector.memset(preload[:, 0:1], 0.0)
-        nc.vector.memset(x_plane[:].bitcast(I32), 0)
-        nc.vector.memset(w_planes[:].bitcast(I32), 0)
+        nc.vector.memset(early_plane[:].bitcast(I32), 0)
+        nc.vector.memset(late_planes[:].bitcast(I32), 0)
         nc.scalar.dma_start(out=scale_window[STAGED, :].bitcast(I32), in_=x_scales[0].bitcast(I32))
         nc.scalar.activation(out=preload[:, 1:2], in_=preload[:, 0:1], func=GELU)
 
         w2_rows = w2.rearrange("(p j) c -> p j c", j=PACK)
         nc.sync.dma_start(offsets[:], offs)
-        for a in range(2):
-            nc.sync.dma_start(out=w2_raw[a][:], in_=w2_rows[:, :, a * HALF_H : (a + 1) * HALF_H])
+        nc.sync.dma_start(out=w2_raw[:], in_=w2_rows)
         nc.sync.dma_start(out=word_window[:].bitcast(I32), in_=words_of(x_words))
-        nc.sync.dma_start(out=w_rows[STAGED, w1_cols].bitcast(I32), in_=w1_scales[0].bitcast(I32))
-        nc.sync.dma_start(out=w_rows[STAGED, w3_cols].bitcast(I32), in_=w3_scales[0].bitcast(I32))
+        nc.sync.dma_start(out=late_rows[STAGED, w1_cols].bitcast(I32), in_=w1_scales[0].bitcast(I32))
+        nc.sync.dma_start(out=late_rows[STAGED, w3_cols].bitcast(I32), in_=w3_scales[0].bitcast(I32))
 
         def place_scales(queue, plane, rows):
             for r in range(4):
                 queue.dma_start(out=plane[r:P:32, :].bitcast(I32), in_=rows[STAGED.start + r : STAGED.stop : 4, :].bitcast(I32))
 
-        nc.vector.tensor_copy(picked_rows[:], scale_window[:].indirect(offsets[:]))
+        nc.vector.tensor_copy(picked_early[:], scale_window[:].indirect(offsets[:, 0 : EARLY // LIST_ROWS]))
+        nc.vector.tensor_copy(picked_late[:], scale_window[:].indirect(offsets[:, EARLY // LIST_ROWS : S // LIST_ROWS]))
         w_words = keep.tile([P, 2 * N], U32, name="w_words", tag="scale_window", align_bytes=64)
         w1_codes = w_words[:, 0:N]
         w3_codes = w_words[:, N : 2 * N]
-        place_scales(nc.sync, x_plane, picked_rows)
+        place_scales(nc.sync, early_plane, picked_early)
         nc.sync.dma_start(out=w1_codes.bitcast(I32), in_=words_of(w1_words))
         nc.sync.dma_start(out=w3_codes.bitcast(I32), in_=words_of(w3_words))
 
-        def regroup(copy, a, first, last):
+        def regroup(copy, first, last, tiles):
             copy(
-                out=w2_bf16[:, :, GROUPS * a + first : GROUPS * a + last, :].rearrange("p t m j -> p m j t"),
-                in_=w2_raw[a][:, :, PACK * first : PACK * last].rearrange("p j (m t) -> p m j t", t=PACK),
+                out=w2_bf16[:, tiles, first:last, :].rearrange("p t m j -> p m j t"),
+                in_=w2_raw[:, :, PACK * first : PACK * last].rearrange("p j (m t) -> p m j t", t=PACK)[:, :, :, tiles],
             )
 
-        regroup(nc.scalar.copy, 0, 0, GROUPS)
-        regroup(nc.scalar.copy, 1, 0, SCALAR_GROUPS)
-        regroup(nc.vector.tensor_copy, 1, SCALAR_GROUPS, GROUPS)
-        place_scales(nc.scalar, w_planes, w_rows)
+        regroup(nc.scalar.copy, 0, SCALAR_GROUPS, slice(0, PACK))
+        regroup(nc.vector.tensor_copy, SCALAR_GROUPS, GROUPS, slice(0, 2))
+        regroup(nc.vector.tensor_copy, SCALAR_GROUPS, GROUPS, slice(2, 4))
+        nc.vector.tensor_copy(out=late_rows[:, 0:LATE].bitcast(I32), in_=picked_late[:].bitcast(I32))
+        place_scales(nc.scalar, late_planes, late_rows)
         for t in range(PACK):
             cols = slice(t * P, (t + 1) * P)
             nc.vector.quantize_mx(out=w2_words[:, cols].bitcast(FP8X4), scales=w2_plane[:, cols], in_=w2_bf16[:, t].rearrange("p m j -> p (m j)"))
@@ -114,7 +116,7 @@ def tile_picked_lora_gelu_p_kernel(tc, x_words, x_scales, w1_words, w1_scales, w
             nc.vector.tensor_copy(x_codes[g][:], word_window[:].indirect(offsets[:, entries]))
 
         out_halves = out.rearrange("(m p) n -> p m n", p=P)
-        results = keep.tile([P, 2, S - CHUNK], F32, name="results", align_bytes=64)
+        results = keep.tile([P, 2, S - 2 * CHUNK], F32, name="results", align_bytes=64)
 
         def tokens(c):
             return slice(c * CHUNK, (c + 1) * CHUNK)
@@ -122,7 +124,9 @@ def tile_picked_lora_gelu_p_kernel(tc, x_words, x_scales, w1_words, w1_scales, w
         def x_operand(c):
             g = max(n for n, at in enumerate(GATHER_AT) if at <= c * CHUNK)
             word_at = c * CHUNK - GATHER_AT[g]
-            return x_codes[g][:, word_at : word_at + CHUNK], x_plane[:, tokens(c)]
+            byte_at = c * CHUNK
+            plane = early_plane[:, byte_at : byte_at + CHUNK] if byte_at < EARLY else late_planes[:, byte_at - EARLY : byte_at - EARLY + CHUNK]
+            return x_codes[g][:, word_at : word_at + CHUNK], plane
 
         def product(dst, codes, plane, block, moving_codes, moving_plane, start, stop):
             cols = slice(block * P, (block + 1) * P)
@@ -157,18 +161,17 @@ def tile_picked_lora_gelu_p_kernel(tc, x_words, x_scales, w1_words, w1_scales, w
                 product(halves[m], w3_codes, w3_plane, m, *h_operand, False, len(OUT_BANKS[c]) == 2 or m == 1)
 
         def drain(c, sums):
-            if c == CHUNKS - 1:
-                last = [keep.tile([P, CHUNK], F32, name=f"last{m}", align_bytes=64) for m in range(2)]
-                nc.scalar.copy(out=last[0][:], in_=sums[0][:])
-                nc.vector.tensor_copy(out=last[1][:], in_=sums[1][:])
-                nc.scalar.dma_start(out=out[0:P, tokens(c)], in_=last[0][:])
-                nc.sync.dma_start(out=out[P : 2 * P, tokens(c)], in_=last[1][:])
+            if len(OUT_BANKS[c]) == 2:
+                halves = [keep.tile([P, CHUNK], F32, name=f"half{c}_{m}", align_bytes=64) for m in range(2)]
+                mine = c % 2
+                other = 1 - mine
+                nc.scalar.copy(out=halves[mine][:], in_=sums[mine][:])
+                nc.vector.tensor_copy(out=halves[other][:], in_=sums[other][:])
+                nc.scalar.dma_start(out=out[mine * P : (mine + 1) * P, tokens(c)], in_=halves[mine][:])
+                nc.sync.dma_start(out=out[other * P : (other + 1) * P, tokens(c)], in_=halves[other][:])
                 return
             result = results[:, :, tokens(c)]
-            if len(OUT_BANKS[c]) == 2:
-                nc.scalar.copy(out=result[:, 0, :], in_=sums[0][:])
-                nc.vector.tensor_copy(out=result[:, 1, :], in_=sums[1][:])
-            elif c == SCALAR_CHUNK:
+            if c == SCALAR_CHUNK:
                 nc.scalar.copy(out=result, in_=sums[:])
             else:
                 nc.vector.tensor_copy(out=result, in_=sums[:])

@@ -1,6 +1,7 @@
 from contextlib import ExitStack
 
 import concourse.mybir as mybir
+from concourse.masks import make_identity
 
 K, T, S, H, N = 512, 2048, 1024, 512, 256
 FLOPS = 2 * S * (K * H + K * N + H * N)
@@ -28,6 +29,7 @@ LATE = S - EARLY
 GROUPS = H // PACK
 SCALAR_GROUPS = 62
 WARM_UP = [128, 128, 256, 256]
+WARM_TRANSPOSES = 8
 H_BANKS = [0, 1, 2, 3, 0, 2, 3, 0]
 H_AHEAD = 5
 OUT_BANKS = [(4,), (5,), (6,), (7,), (1,), (4,), (5, 2), (6, 3)]
@@ -66,6 +68,8 @@ def tile_picked_lora_gelu_p_kernel(tc, x_words, x_scales, w1_words, w1_scales, w
         picked_late = keep.tile([P, LATE], U8, name="picked_late", align_bytes=64)
         x_codes = [keep.tile([P, width], U32, name=f"x_codes{g}", align_bytes=64) for g, width in enumerate(GATHERS)]
 
+        identity = keep.tile([P, P], F32, name="identity", align_bytes=64)
+        make_identity(nc, identity[:])
         for rows in (slice(0, STAGED.start), slice(STAGED.stop, 64), slice(64, P)):
             nc.vector.memset(scale_window[rows, :].bitcast(I32), 0)
         nc.vector.memset(preload[:, 0:1], 0.0)
@@ -85,6 +89,9 @@ def tile_picked_lora_gelu_p_kernel(tc, x_words, x_scales, w1_words, w1_scales, w
             for r in range(4):
                 queue.dma_start(out=plane[r:P:32, :].bitcast(I32), in_=rows[STAGED.start + r : STAGED.stop : 4, :].bitcast(I32))
 
+        scrap = psum.tile([P, 4 * P], F32, name="scrap", tag="bank7")
+        for n in range(WARM_TRANSPOSES):
+            nc.tensor.transpose(scrap[:, (n % 4) * P : (n % 4 + 1) * P], w2_raw[:, n % 4, (n // 4) * P : (n // 4 + 1) * P], identity[:])
         nc.vector.tensor_copy(picked_early[:], scale_window[:].indirect(offsets[:, 0 : EARLY // LIST_ROWS]))
         nc.vector.tensor_copy(picked_late[:], scale_window[:].indirect(offsets[:, EARLY // LIST_ROWS : S // LIST_ROWS]))
         w_words = keep.tile([P, 2 * N], U32, name="w_words", tag="scale_window", align_bytes=64)
@@ -108,7 +115,6 @@ def tile_picked_lora_gelu_p_kernel(tc, x_words, x_scales, w1_words, w1_scales, w
         for t in range(PACK):
             cols = slice(t * P, (t + 1) * P)
             nc.vector.quantize_mx(out=w2_words[:, cols].bitcast(FP8X4), scales=w2_plane[:, cols], in_=w2_bf16[:, t].rearrange("p m j -> p (m j)"))
-        scrap = psum.tile([P, 4 * P], F32, name="scrap", tag="bank7")
         for width in WARM_UP:
             nc.tensor.matmul_mx(out=scrap[:, 0:width], lhsT=w2_words[:, 0:P].bitcast(FP8X4), lhsT_scale=w2_plane[:, 0:P], rhs=w2_words[:, 0:width].bitcast(FP8X4), rhs_scale=w2_plane[:, 0:width], start=True, stop=True)
         for g, width in enumerate(GATHERS):

@@ -26,10 +26,9 @@ CHUNK = 128
 CHUNKS = S // CHUNK
 EARLY = 6 * CHUNK
 LATE = S - EARLY
-GROUPS = H // PACK
-SCALAR_GROUPS = 62
-WARM_UP = [128, 128, 256, 256]
-WARM_TRANSPOSES = 8
+HALF = 64
+WARM_UP = [256, 256, 128]
+WARM_TRANSPOSES = 5
 H_BANKS = [0, 1, 2, 3, 0, 2, 3, 0]
 H_AHEAD = 5
 OUT_BANKS = [(4,), (5,), (6,), (7,), (1,), (4,), (5, 2), (6, 3)]
@@ -53,7 +52,7 @@ def tile_picked_lora_gelu_p_kernel(tc, x_words, x_scales, w1_words, w1_scales, w
         scale_window = keep.tile([P, T], U8, name="scale_window", tag="scale_window", align_bytes=64)
         word_window = keep.tile([P, T], U32, name="word_window", align_bytes=64)
         w2_raw = keep.tile([P, PACK, H], F32, name="w2_raw", align_bytes=64)
-        w2_bf16 = keep.tile([P, PACK, P, PACK], BF16, name="w2_bf16", align_bytes=64)
+        w2_bf16 = [[keep.tile([P, 2, HALF, PACK], BF16, name=f"w2_bf16_{a}{u}", align_bytes=64) for u in range(2)] for a in range(2)]
         w2_words = keep.tile([P, H], U32, name="w2_words", align_bytes=64)
         w2_plane = keep.tile([P, H], U8, name="w2_plane", align_bytes=64)
         preload = keep.tile([P, 2], F32, name="preload", align_bytes=64)
@@ -89,9 +88,6 @@ def tile_picked_lora_gelu_p_kernel(tc, x_words, x_scales, w1_words, w1_scales, w
             for r in range(4):
                 queue.dma_start(out=plane[r:P:32, :].bitcast(I32), in_=rows[STAGED.start + r : STAGED.stop : 4, :].bitcast(I32))
 
-        scrap = psum.tile([P, 4 * P], F32, name="scrap", tag="bank7")
-        for n in range(WARM_TRANSPOSES):
-            nc.tensor.transpose(scrap[:, (n % 4) * P : (n % 4 + 1) * P], w2_raw[:, n % 4, (n // 4) * P : (n // 4 + 1) * P], identity[:])
         nc.vector.tensor_copy(picked_early[:], scale_window[:].indirect(offsets[:, 0 : EARLY // LIST_ROWS]))
         nc.vector.tensor_copy(picked_late[:], scale_window[:].indirect(offsets[:, EARLY // LIST_ROWS : S // LIST_ROWS]))
         w_words = keep.tile([P, 2 * N], U32, name="w_words", tag="scale_window", align_bytes=64)
@@ -101,20 +97,21 @@ def tile_picked_lora_gelu_p_kernel(tc, x_words, x_scales, w1_words, w1_scales, w
         nc.sync.dma_start(out=w1_codes.bitcast(I32), in_=words_of(w1_words))
         nc.sync.dma_start(out=w3_codes.bitcast(I32), in_=words_of(w3_words))
 
-        def regroup(copy, first, last, tiles):
-            copy(
-                out=w2_bf16[:, tiles, first:last, :].rearrange("p t m j -> p m j t"),
-                in_=w2_raw[:, :, PACK * first : PACK * last].rearrange("p j (m t) -> p m j t", t=PACK)[:, :, :, tiles],
-            )
-
-        regroup(nc.scalar.copy, 0, SCALAR_GROUPS, slice(0, PACK))
-        regroup(nc.vector.tensor_copy, SCALAR_GROUPS, GROUPS, slice(0, 2))
-        regroup(nc.vector.tensor_copy, SCALAR_GROUPS, GROUPS, slice(2, 4))
+        w2_groups = w2_raw[:].rearrange("p j (m t) -> p m j t", t=PACK)
+        for u in range(2):
+            for a, copy in enumerate((nc.scalar.copy, nc.vector.tensor_copy)):
+                copy(out=w2_bf16[a][u][:].rearrange("p e m j -> p m j e"), in_=w2_groups[:, a * HALF : (a + 1) * HALF, :, 2 * u : 2 * u + 2])
+        scrap = psum.tile([P, 4 * P], F32, name="scrap", tag="bank7")
+        pairs = w2_bf16[0][0][:, 0].rearrange("p m j -> p (m j)").bitcast(F32)
+        for n in range(WARM_TRANSPOSES):
+            nc.tensor.transpose(scrap[:, (n % PACK) * P : (n % PACK + 1) * P], pairs, identity[:])
         nc.vector.tensor_copy(out=late_rows[:, 0:LATE].bitcast(I32), in_=picked_late[:].bitcast(I32))
         place_scales(nc.scalar, late_planes, late_rows)
-        for t in range(PACK):
-            cols = slice(t * P, (t + 1) * P)
-            nc.vector.quantize_mx(out=w2_words[:, cols].bitcast(FP8X4), scales=w2_plane[:, cols], in_=w2_bf16[:, t].rearrange("p m j -> p (m j)"))
+        for u, a in ((0, 0), (0, 1), (1, 1), (1, 0)):
+            for e in range(2):
+                first = (2 * u + e) * P + a * HALF
+                cols = slice(first, first + HALF)
+                nc.vector.quantize_mx(out=w2_words[:, cols].bitcast(FP8X4), scales=w2_plane[:, cols], in_=w2_bf16[a][u][:, e].rearrange("p m j -> p (m j)"))
         for width in WARM_UP:
             nc.tensor.matmul_mx(out=scrap[:, 0:width], lhsT=w2_words[:, 0:P].bitcast(FP8X4), lhsT_scale=w2_plane[:, 0:P], rhs=w2_words[:, 0:width].bitcast(FP8X4), rhs_scale=w2_plane[:, 0:width], start=True, stop=True)
         for g, width in enumerate(GATHERS):

@@ -16,6 +16,7 @@ FP8X4 = mybir.dt.float8_e4m3fn_x4
 GELU = mybir.ActivationFunctionType.Gelu_apprx_tanh
 
 P = 128
+MX_ALIGN = 256
 PACK = 4
 LIST_ROWS = 16
 BLOCKS = 16
@@ -49,15 +50,15 @@ def tile_picked_lora_gelu_p_kernel(tc, x_words, x_scales, w1_words, w1_scales, w
         psum = ctx.enter_context(tc.psum_pool(name="psum", bufs=1))
 
         offsets = keep.tile([P, S // LIST_ROWS], U16, name="offsets")
-        scale_window = keep.tile([P, T], U8, name="scale_window", tag="scale_window", align_bytes=64)
+        scale_window = keep.tile([P, T], U8, name="scale_window", tag="scale_window", align_bytes=MX_ALIGN)
         word_window = keep.tile([P, T], U32, name="word_window", align_bytes=64)
         w2_raw = keep.tile([P, PACK, H], F32, name="w2_raw", align_bytes=64)
         w2_bf16 = [[keep.tile([P, 2, HALF, PACK], BF16, name=f"w2_bf16_{a}{u}", align_bytes=64) for u in range(2)] for a in range(2)]
-        w2_words = keep.tile([P, H], U32, name="w2_words", align_bytes=64)
-        w2_plane = keep.tile([P, H], U8, name="w2_plane", align_bytes=64)
+        w2_words = keep.tile([P, H], U32, name="w2_words", align_bytes=MX_ALIGN)
+        w2_plane = keep.tile([P, H], U8, name="w2_plane", align_bytes=MX_ALIGN)
         preload = keep.tile([P, 2], F32, name="preload", align_bytes=64)
-        early_plane = keep.tile([P, EARLY], U8, name="early_plane", align_bytes=64)
-        late_planes = keep.tile([P, LATE + 2 * N], U8, name="late_planes", align_bytes=64)
+        early_plane = keep.tile([P, EARLY], U8, name="early_plane", align_bytes=MX_ALIGN)
+        late_planes = keep.tile([P, LATE + 2 * N], U8, name="late_planes", align_bytes=MX_ALIGN)
         late_rows = keep.tile([P, LATE + 2 * N], U8, name="late_rows", align_bytes=64)
         w1_cols = slice(LATE, LATE + N)
         w3_cols = slice(LATE + N, LATE + 2 * N)
@@ -65,7 +66,7 @@ def tile_picked_lora_gelu_p_kernel(tc, x_words, x_scales, w1_words, w1_scales, w
         w3_plane = late_planes[:, w3_cols]
         picked_early = keep.tile([P, EARLY], U8, name="picked_early", align_bytes=64)
         picked_late = keep.tile([P, LATE], U8, name="picked_late", align_bytes=64)
-        x_codes = [keep.tile([P, width], U32, name=f"x_codes{g}", align_bytes=64) for g, width in enumerate(GATHERS)]
+        x_codes = [keep.tile([P, width], U32, name=f"x_codes{g}", align_bytes=MX_ALIGN) for g, width in enumerate(GATHERS)]
 
         identity = keep.tile([P, P], F32, name="identity", align_bytes=64)
         make_identity(nc, identity[:])
@@ -90,7 +91,7 @@ def tile_picked_lora_gelu_p_kernel(tc, x_words, x_scales, w1_words, w1_scales, w
 
         nc.vector.tensor_copy(picked_early[:], scale_window[:].indirect(offsets[:, 0 : EARLY // LIST_ROWS]))
         nc.vector.tensor_copy(picked_late[:], scale_window[:].indirect(offsets[:, EARLY // LIST_ROWS : S // LIST_ROWS]))
-        w_words = keep.tile([P, 2 * N], U32, name="w_words", tag="scale_window", align_bytes=64)
+        w_words = keep.tile([P, 2 * N], U32, name="w_words", tag="scale_window", align_bytes=MX_ALIGN)
         w1_codes = w_words[:, 0:N]
         w3_codes = w_words[:, N : 2 * N]
         place_scales(nc.sync, early_plane, picked_early)
@@ -156,8 +157,8 @@ def tile_picked_lora_gelu_p_kernel(tc, x_words, x_scales, w1_words, w1_scales, w
             return tiles, halves
 
         def close_sums(c, h_bf16, halves):
-            h_words = keep.tile([P, CHUNK], U32, name="h_words", tag=f"h_words{H_CODE_BUFFERS[c]}", align_bytes=64)
-            h_plane = keep.tile([P, CHUNK], U8, name="h_plane", tag=f"h_plane{H_CODE_BUFFERS[c]}", align_bytes=64)
+            h_words = keep.tile([P, CHUNK], U32, name="h_words", tag=f"h_words{H_CODE_BUFFERS[c]}", align_bytes=MX_ALIGN)
+            h_plane = keep.tile([P, CHUNK], U8, name="h_plane", tag=f"h_plane{H_CODE_BUFFERS[c]}", align_bytes=MX_ALIGN)
             h_operand = (h_words[:], h_plane[:])
             nc.vector.quantize_mx(out=h_operand[0].bitcast(FP8X4), scales=h_operand[1], in_=h_bf16[:].rearrange("p n t -> p (n t)"))
             for m in range(2):

@@ -16,7 +16,7 @@ FP8X4 = mybir.dt.float8_e4m3fn_x4
 GELU = mybir.ActivationFunctionType.Gelu_apprx_tanh
 
 P = 128
-MX_ALIGN = 256
+ALIGN = 256
 PACK = 4
 LIST_ROWS = 16
 BLOCKS = 16
@@ -49,26 +49,26 @@ def tile_picked_lora_gelu_p_kernel(tc, x_words, x_scales, w1_words, w1_scales, w
         keep = ctx.enter_context(tc.tile_pool(name="keep", bufs=1))
         psum = ctx.enter_context(tc.psum_pool(name="psum", bufs=1))
 
-        offsets = keep.tile([P, S // LIST_ROWS], U16, name="offsets")
-        scale_window = keep.tile([P, T], U8, name="scale_window", tag="scale_window", align_bytes=MX_ALIGN)
-        word_window = keep.tile([P, T], U32, name="word_window", align_bytes=64)
-        w2_raw = keep.tile([P, PACK, H], F32, name="w2_raw", align_bytes=64)
-        w2_bf16 = [[keep.tile([P, 2, HALF, PACK], BF16, name=f"w2_bf16_{a}{u}", align_bytes=64) for u in range(2)] for a in range(2)]
-        w2_words = keep.tile([P, H], U32, name="w2_words", align_bytes=MX_ALIGN)
-        w2_plane = keep.tile([P, H], U8, name="w2_plane", align_bytes=MX_ALIGN)
-        preload = keep.tile([P, 2], F32, name="preload", align_bytes=64)
-        early_plane = keep.tile([P, EARLY], U8, name="early_plane", align_bytes=MX_ALIGN)
-        late_planes = keep.tile([P, LATE + 2 * N], U8, name="late_planes", align_bytes=MX_ALIGN)
-        late_rows = keep.tile([P, LATE + 2 * N], U8, name="late_rows", align_bytes=64)
+        offsets = keep.tile([P, S // LIST_ROWS], U16, name="offsets", align_bytes=ALIGN)
+        scale_window = keep.tile([P, T], U8, name="scale_window", tag="scale_window", align_bytes=ALIGN)
+        word_window = keep.tile([P, T], U32, name="word_window", align_bytes=ALIGN)
+        w2_raw = keep.tile([P, PACK, H], F32, name="w2_raw", align_bytes=ALIGN)
+        w2_bf16 = [[keep.tile([P, 2, HALF, PACK], BF16, name=f"w2_bf16_{a}{u}", align_bytes=ALIGN) for u in range(2)] for a in range(2)]
+        w2_words = keep.tile([P, H], U32, name="w2_words", align_bytes=ALIGN)
+        w2_plane = keep.tile([P, H], U8, name="w2_plane", align_bytes=ALIGN)
+        preload = keep.tile([P, 2], F32, name="preload", align_bytes=ALIGN)
+        early_plane = keep.tile([P, EARLY], U8, name="early_plane", align_bytes=ALIGN)
+        late_planes = keep.tile([P, LATE + 2 * N], U8, name="late_planes", align_bytes=ALIGN)
+        late_rows = keep.tile([P, LATE + 2 * N], U8, name="late_rows", align_bytes=ALIGN)
         w1_cols = slice(LATE, LATE + N)
         w3_cols = slice(LATE + N, LATE + 2 * N)
         w1_plane = late_planes[:, w1_cols]
         w3_plane = late_planes[:, w3_cols]
-        picked_early = keep.tile([P, EARLY], U8, name="picked_early", align_bytes=64)
-        picked_late = keep.tile([P, LATE], U8, name="picked_late", align_bytes=64)
-        x_codes = [keep.tile([P, width], U32, name=f"x_codes{g}", align_bytes=MX_ALIGN) for g, width in enumerate(GATHERS)]
+        picked_early = keep.tile([P, EARLY], U8, name="picked_early", align_bytes=ALIGN)
+        picked_late = keep.tile([P, LATE], U8, name="picked_late", align_bytes=ALIGN)
+        x_codes = [keep.tile([P, width], U32, name=f"x_codes{g}", align_bytes=ALIGN) for g, width in enumerate(GATHERS)]
 
-        identity = keep.tile([P, P], F32, name="identity", align_bytes=64)
+        identity = keep.tile([P, P], F32, name="identity", align_bytes=ALIGN)
         make_identity(nc, identity[:])
         for rows in (slice(0, STAGED.start), slice(STAGED.stop, 64), slice(64, P)):
             nc.vector.memset(scale_window[rows, :].bitcast(I32), 0)
@@ -91,7 +91,7 @@ def tile_picked_lora_gelu_p_kernel(tc, x_words, x_scales, w1_words, w1_scales, w
 
         nc.vector.tensor_copy(picked_early[:], scale_window[:].indirect(offsets[:, 0 : EARLY // LIST_ROWS]))
         nc.vector.tensor_copy(picked_late[:], scale_window[:].indirect(offsets[:, EARLY // LIST_ROWS : S // LIST_ROWS]))
-        w_words = keep.tile([P, 2 * N], U32, name="w_words", tag="scale_window", align_bytes=MX_ALIGN)
+        w_words = keep.tile([P, 2 * N], U32, name="w_words", tag="scale_window", align_bytes=ALIGN)
         w1_codes = w_words[:, 0:N]
         w3_codes = w_words[:, N : 2 * N]
         place_scales(nc.sync, early_plane, picked_early)
@@ -120,7 +120,7 @@ def tile_picked_lora_gelu_p_kernel(tc, x_words, x_scales, w1_words, w1_scales, w
             nc.vector.tensor_copy(x_codes[g][:], word_window[:].indirect(offsets[:, entries]))
 
         out_halves = out.rearrange("(m p) n -> p m n", p=P)
-        results = keep.tile([P, 2, S - 2 * CHUNK], F32, name="results", align_bytes=64)
+        results = keep.tile([P, 2, S - 2 * CHUNK], F32, name="results", align_bytes=ALIGN)
 
         def tokens(c):
             return slice(c * CHUNK, (c + 1) * CHUNK)
@@ -140,7 +140,7 @@ def tile_picked_lora_gelu_p_kernel(tc, x_words, x_scales, w1_words, w1_scales, w
             bank = psum.tile([P, PACK, CHUNK], F32, name="h_sums", tag=f"bank{H_BANKS[c]}")
             for t in range(PACK):
                 product(bank[:, t, :], w2_words, w2_plane, t, *x_operand(c), True, True)
-            h_bf16 = keep.tile([P, CHUNK, PACK], BF16, name=f"h_bf16_{c}", align_bytes=64)
+            h_bf16 = keep.tile([P, CHUNK, PACK], BF16, name=f"h_bf16_{c}", align_bytes=ALIGN)
             nc.scalar.activation(out=h_bf16[:], in_=bank[:].rearrange("p t n -> p n t"), func=GELU)
             return h_bf16
 
@@ -157,8 +157,8 @@ def tile_picked_lora_gelu_p_kernel(tc, x_words, x_scales, w1_words, w1_scales, w
             return tiles, halves
 
         def close_sums(c, h_bf16, halves):
-            h_words = keep.tile([P, CHUNK], U32, name="h_words", tag=f"h_words{H_CODE_BUFFERS[c]}", align_bytes=MX_ALIGN)
-            h_plane = keep.tile([P, CHUNK], U8, name="h_plane", tag=f"h_plane{H_CODE_BUFFERS[c]}", align_bytes=MX_ALIGN)
+            h_words = keep.tile([P, CHUNK], U32, name="h_words", tag=f"h_words{H_CODE_BUFFERS[c]}", align_bytes=ALIGN)
+            h_plane = keep.tile([P, CHUNK], U8, name="h_plane", tag=f"h_plane{H_CODE_BUFFERS[c]}", align_bytes=ALIGN)
             h_operand = (h_words[:], h_plane[:])
             nc.vector.quantize_mx(out=h_operand[0].bitcast(FP8X4), scales=h_operand[1], in_=h_bf16[:].rearrange("p n t -> p (n t)"))
             for m in range(2):
@@ -166,7 +166,7 @@ def tile_picked_lora_gelu_p_kernel(tc, x_words, x_scales, w1_words, w1_scales, w
 
         def drain(c, sums):
             if len(OUT_BANKS[c]) == 2:
-                halves = [keep.tile([P, CHUNK], F32, name=f"half{c}_{m}", align_bytes=64) for m in range(2)]
+                halves = [keep.tile([P, CHUNK], F32, name=f"half{c}_{m}", align_bytes=ALIGN) for m in range(2)]
                 mine = c % 2
                 other = 1 - mine
                 nc.scalar.copy(out=halves[mine][:], in_=sums[mine][:])

@@ -25,7 +25,7 @@ GATHERS = [128, 128, 256, 256, 256]
 GATHER_AT = [sum(GATHERS[:g]) for g in range(len(GATHERS))]
 CHUNK = 128
 CHUNKS = S // CHUNK
-EARLY = 6 * CHUNK
+EARLY = 5 * CHUNK
 LATE = S - EARLY
 HALF = 64
 WARM_UP = [256, 256, 128]
@@ -36,7 +36,7 @@ OUT_BANKS = [(4,), (5,), (6,), (7,), (1,), (4,), (5, 2), (6, 3)]
 SCALAR_CHUNK = 5
 STORE_FROM = {1: 0, 3: 2, 4: 4, 5: 5}
 DRAIN_LAG = 2
-H_CODE_BUFFERS = [0, 1, 2, 3, 4, 3, 4, 5]
+H_CODE_BUFFERS = [0, 1, 2, 0, 1, 0, 1, 2]
 
 
 def words_of(dram):
@@ -52,14 +52,13 @@ def tile_picked_lora_gelu_p_kernel(tc, x_words, x_scales, w1_words, w1_scales, w
         offsets = keep.tile([P, S // LIST_ROWS], U16, name="offsets", align_bytes=ALIGN)
         scale_window = keep.tile([P, T], U8, name="scale_window", tag="scale_window", align_bytes=ALIGN)
         word_window = keep.tile([P, T], U32, name="word_window", align_bytes=ALIGN)
-        w2_raw = keep.tile([P, PACK, H], F32, name="w2_raw", align_bytes=ALIGN)
+        w2_raw = keep.tile([P, PACK, H], F32, name="w2_raw", tag="w2_raw", align_bytes=ALIGN)
         w2_bf16 = [[keep.tile([P, 2, HALF, PACK], BF16, name=f"w2_bf16_{a}{u}", align_bytes=ALIGN) for u in range(2)] for a in range(2)]
         w2_words = keep.tile([P, H], U32, name="w2_words", align_bytes=ALIGN)
         w2_plane = keep.tile([P, H], U8, name="w2_plane", align_bytes=ALIGN)
         preload = keep.tile([P, 2], F32, name="preload", align_bytes=ALIGN)
         early_plane = keep.tile([P, EARLY], U8, name="early_plane", align_bytes=ALIGN)
         late_planes = keep.tile([P, LATE + 2 * N], U8, name="late_planes", align_bytes=ALIGN)
-        late_rows = keep.tile([P, LATE + 2 * N], U8, name="late_rows", align_bytes=ALIGN)
         w1_cols = slice(LATE, LATE + N)
         w3_cols = slice(LATE + N, LATE + 2 * N)
         w1_plane = late_planes[:, w1_cols]
@@ -82,32 +81,33 @@ def tile_picked_lora_gelu_p_kernel(tc, x_words, x_scales, w1_words, w1_scales, w
         nc.sync.dma_start(offsets[:], offs)
         nc.sync.dma_start(out=w2_raw[:], in_=w2_rows)
         nc.sync.dma_start(out=word_window[:].bitcast(I32), in_=words_of(x_words))
-        nc.sync.dma_start(out=late_rows[STAGED, w1_cols].bitcast(I32), in_=w1_scales[0].bitcast(I32))
-        nc.sync.dma_start(out=late_rows[STAGED, w3_cols].bitcast(I32), in_=w3_scales[0].bitcast(I32))
 
-        def place_scales(queue, plane, rows):
+        def place_scales(plane, rows):
             for r in range(4):
-                queue.dma_start(out=plane[r:P:32, :].bitcast(I32), in_=rows[STAGED.start + r : STAGED.stop : 4, :].bitcast(I32))
+                nc.sync.dma_start(out=plane[r:P:32, :].bitcast(I32), in_=rows[STAGED.start + r : STAGED.stop : 4, :].bitcast(I32))
 
         nc.vector.tensor_copy(picked_early[:], scale_window[:].indirect(offsets[:, 0 : EARLY // LIST_ROWS]))
         nc.vector.tensor_copy(picked_late[:], scale_window[:].indirect(offsets[:, EARLY // LIST_ROWS : S // LIST_ROWS]))
-        w_words = keep.tile([P, 2 * N], U32, name="w_words", tag="scale_window", align_bytes=ALIGN)
-        w1_codes = w_words[:, 0:N]
-        w3_codes = w_words[:, N : 2 * N]
-        place_scales(nc.sync, early_plane, picked_early)
-        nc.sync.dma_start(out=w1_codes.bitcast(I32), in_=words_of(w1_words))
-        nc.sync.dma_start(out=w3_codes.bitcast(I32), in_=words_of(w3_words))
+        place_scales(early_plane, picked_early)
+        late_rows = keep.tile([P, LATE + 2 * N], U8, name="late_rows", tag="scale_window", align_bytes=ALIGN)
+        nc.sync.dma_start(out=late_rows[STAGED, w1_cols].bitcast(I32), in_=w1_scales[0].bitcast(I32))
+        nc.sync.dma_start(out=late_rows[STAGED, w3_cols].bitcast(I32), in_=w3_scales[0].bitcast(I32))
 
         w2_groups = w2_raw[:].rearrange("p j (m t) -> p m j t", t=PACK)
         for u in range(2):
             for a, copy in enumerate((nc.scalar.copy, nc.vector.tensor_copy)):
                 copy(out=w2_bf16[a][u][:].rearrange("p e m j -> p m j e"), in_=w2_groups[:, a * HALF : (a + 1) * HALF, :, 2 * u : 2 * u + 2])
+        w_words = keep.tile([P, 2 * N], U32, name="w_words", tag="w2_raw", align_bytes=ALIGN)
+        w1_codes = w_words[:, 0:N]
+        w3_codes = w_words[:, N : 2 * N]
+        nc.sync.dma_start(out=w1_codes.bitcast(I32), in_=words_of(w1_words))
+        nc.sync.dma_start(out=w3_codes.bitcast(I32), in_=words_of(w3_words))
         scrap = psum.tile([P, 4 * P], F32, name="scrap", tag="bank7")
         pairs = w2_bf16[0][0][:, 0].rearrange("p m j -> p (m j)").bitcast(F32)
         for n in range(WARM_TRANSPOSES):
             nc.tensor.transpose(scrap[:, (n % PACK) * P : (n % PACK + 1) * P], pairs, identity[:])
         nc.vector.tensor_copy(out=late_rows[:, 0:LATE].bitcast(I32), in_=picked_late[:].bitcast(I32))
-        place_scales(nc.scalar, late_planes, late_rows)
+        place_scales(late_planes, late_rows)
         for u, a in ((0, 0), (0, 1), (1, 1), (1, 0)):
             for e in range(2):
                 first = (2 * u + e) * P + a * HALF
@@ -126,34 +126,38 @@ def tile_picked_lora_gelu_p_kernel(tc, x_words, x_scales, w1_words, w1_scales, w
             return slice(c * CHUNK, (c + 1) * CHUNK)
 
         def x_operand(c):
+            width = CHUNK
             g = max(n for n, at in enumerate(GATHER_AT) if at <= c * CHUNK)
             word_at = c * CHUNK - GATHER_AT[g]
             byte_at = c * CHUNK
-            plane = early_plane[:, byte_at : byte_at + CHUNK] if byte_at < EARLY else late_planes[:, byte_at - EARLY : byte_at - EARLY + CHUNK]
-            return x_codes[g][:, word_at : word_at + CHUNK], plane
+            plane = early_plane[:, byte_at : byte_at + width] if byte_at < EARLY else late_planes[:, byte_at - EARLY : byte_at - EARLY + width]
+            return x_codes[g][:, word_at : word_at + width], plane
 
         def product(dst, codes, plane, block, moving_codes, moving_plane, start, stop):
             cols = slice(block * P, (block + 1) * P)
             nc.tensor.matmul_mx(out=dst, lhsT=codes[:, cols].bitcast(FP8X4), lhsT_scale=plane[:, cols], rhs=moving_codes.bitcast(FP8X4), rhs_scale=moving_plane, start=start, stop=stop)
 
+        def activate(c, sums):
+            h_bf16 = keep.tile([P, CHUNK, PACK], BF16, name=f"h_bf16_{c}", align_bytes=ALIGN)
+            nc.scalar.activation(out=h_bf16[:], in_=sums.rearrange("p t n -> p n t"), func=GELU)
+            return h_bf16
+
         def hidden(c):
             bank = psum.tile([P, PACK, CHUNK], F32, name="h_sums", tag=f"bank{H_BANKS[c]}")
             for t in range(PACK):
                 product(bank[:, t, :], w2_words, w2_plane, t, *x_operand(c), True, True)
-            h_bf16 = keep.tile([P, CHUNK, PACK], BF16, name=f"h_bf16_{c}", align_bytes=ALIGN)
-            nc.scalar.activation(out=h_bf16[:], in_=bank[:].rearrange("p t n -> p n t"), func=GELU)
-            return h_bf16
+            return activate(c, bank[:])
 
         def open_sums(c):
             banks = OUT_BANKS[c]
             if len(banks) == 2:
-                tiles = [psum.tile([P, CHUNK], F32, name=f"out_half{m}", tag=f"bank{banks[m]}") for m in range(2)]
-                halves = [tile[:] for tile in tiles]
+                tiles = [psum.tile([P, CHUNK], F32, name=f"out_half{m}", tag=f"bank{banks[m]}")[:] for m in range(2)]
+                halves = tiles
             else:
                 tiles = psum.tile([P, 2, CHUNK], F32, name="out_both", tag=f"bank{banks[0]}")
                 halves = [tiles[:, m, :] for m in range(2)]
             for m in range(2):
-                product(halves[m], w1_codes, w1_plane, m, *x_operand(c), len(banks) == 2 or m == 0, False)
+                product(halves[m], w1_codes, w1_plane, m, *x_operand(c), c >= CHUNKS - 2 or m == 0, False)
             return tiles, halves
 
         def close_sums(c, h_bf16, halves):
@@ -162,15 +166,15 @@ def tile_picked_lora_gelu_p_kernel(tc, x_words, x_scales, w1_words, w1_scales, w
             h_operand = (h_words[:], h_plane[:])
             nc.vector.quantize_mx(out=h_operand[0].bitcast(FP8X4), scales=h_operand[1], in_=h_bf16[:].rearrange("p n t -> p (n t)"))
             for m in range(2):
-                product(halves[m], w3_codes, w3_plane, m, *h_operand, False, len(OUT_BANKS[c]) == 2 or m == 1)
+                product(halves[m], w3_codes, w3_plane, m, *h_operand, False, c >= CHUNKS - 2 or m == 1)
 
         def drain(c, sums):
-            if len(OUT_BANKS[c]) == 2:
+            if c >= CHUNKS - 2:
                 halves = [keep.tile([P, CHUNK], F32, name=f"half{c}_{m}", align_bytes=ALIGN) for m in range(2)]
                 mine = c % 2
                 other = 1 - mine
-                nc.scalar.copy(out=halves[mine][:], in_=sums[mine][:])
-                nc.vector.tensor_copy(out=halves[other][:], in_=sums[other][:])
+                nc.scalar.copy(out=halves[mine][:], in_=sums[mine])
+                nc.vector.tensor_copy(out=halves[other][:], in_=sums[other])
                 nc.scalar.dma_start(out=out[mine * P : (mine + 1) * P, tokens(c)], in_=halves[mine][:])
                 nc.sync.dma_start(out=out[other * P : (other + 1) * P, tokens(c)], in_=halves[other][:])
                 return

@@ -36,7 +36,7 @@ OUT_BANKS = [(4,), (5,), (6,), (7,), (1,), (4,), (5, 2), (6, 3)]
 SCALAR_CHUNK = 5
 STORE_FROM = {1: 0, 3: 2, 4: 4, 5: 5}
 DRAIN_LAG = 2
-H_CODE_BUFFERS = [0, 1, 2, 0, 1, 0, 1, 2]
+H_CODE_BUFFERS = [0, 1, 2, 0, 1, 0, 2, 1]
 
 
 def words_of(dram):
@@ -125,6 +125,10 @@ def tile_picked_lora_gelu_p_kernel(tc, x_words, x_scales, w1_words, w1_scales, w
         def tokens(c):
             return slice(c * CHUNK, (c + 1) * CHUNK)
 
+        def steps(c):
+            width = CHUNK // 2 if c == CHUNKS - 1 else CHUNK
+            return [slice(at, at + width) for at in range(0, CHUNK, width)]
+
         def x_operand(c):
             width = CHUNK
             g = max(n for n, at in enumerate(GATHER_AT) if at <= c * CHUNK)
@@ -139,7 +143,8 @@ def tile_picked_lora_gelu_p_kernel(tc, x_words, x_scales, w1_words, w1_scales, w
 
         def activate(c, sums):
             h_bf16 = keep.tile([P, CHUNK, PACK], BF16, name=f"h_bf16_{c}", align_bytes=ALIGN)
-            nc.scalar.activation(out=h_bf16[:], in_=sums.rearrange("p t n -> p n t"), func=GELU)
+            for part in steps(c):
+                nc.scalar.activation(out=h_bf16[:, part], in_=sums[:, :, part].rearrange("p t n -> p n t"), func=GELU)
             return h_bf16
 
         def hidden(c):
@@ -164,7 +169,8 @@ def tile_picked_lora_gelu_p_kernel(tc, x_words, x_scales, w1_words, w1_scales, w
             h_words = keep.tile([P, CHUNK], U32, name="h_words", tag=f"h_words{H_CODE_BUFFERS[c]}", align_bytes=ALIGN)
             h_plane = keep.tile([P, CHUNK], U8, name="h_plane", tag=f"h_plane{H_CODE_BUFFERS[c]}", align_bytes=ALIGN)
             h_operand = (h_words[:], h_plane[:])
-            nc.vector.quantize_mx(out=h_operand[0].bitcast(FP8X4), scales=h_operand[1], in_=h_bf16[:].rearrange("p n t -> p (n t)"))
+            for part in steps(c):
+                nc.vector.quantize_mx(out=h_words[:, part].bitcast(FP8X4), scales=h_plane[:, part], in_=h_bf16[:, part].rearrange("p n t -> p (n t)"))
             for m in range(2):
                 product(halves[m], w3_codes, w3_plane, m, *h_operand, False, c >= CHUNKS - 2 or m == 1)
 

@@ -34,9 +34,9 @@ H_BANKS = [0, 1, 2, 3, 0, 2, 3, 0]
 H_AHEAD = 5
 OUT_BANKS = [(4,), (5,), (6,), (7,), (1,), (4,), (5, 2), (6, 3)]
 SCALAR_CHUNK = 5
-STORE_FROM = {1: 0, 3: 2, 4: 4, 5: 5}
-DRAIN_LAG = 2
-H_CODE_BUFFERS = [0, 1, 2, 0, 1, 0, 2, 1]
+STORE_FROM = {1: 0, 2: 2, 3: 3, 4: 4, 5: 5, 6: 6}
+DRAIN_LAG = 3
+H_CODE_BUFFERS = [0, 1, 2, 0, 1, 2, 0, 1]
 
 
 def words_of(dram):
@@ -120,7 +120,7 @@ def tile_picked_lora_gelu_p_kernel(tc, x_words, x_scales, w1_words, w1_scales, w
             nc.vector.tensor_copy(x_codes[g][:], word_window[:].indirect(offsets[:, entries]))
 
         out_halves = out.rearrange("(m p) n -> p m n", p=P)
-        results = keep.tile([P, 2, S - 2 * CHUNK], F32, name="results", align_bytes=ALIGN)
+        results = keep.tile([P, 2, S - CHUNK], F32, name="results", align_bytes=ALIGN)
 
         def tokens(c):
             return slice(c * CHUNK, (c + 1) * CHUNK)
@@ -175,23 +175,25 @@ def tile_picked_lora_gelu_p_kernel(tc, x_words, x_scales, w1_words, w1_scales, w
                 product(halves[m], w3_codes, w3_plane, m, *h_operand, False, c >= CHUNKS - 2 or m == 1)
 
         def drain(c, sums):
-            if c >= CHUNKS - 2:
-                halves = [keep.tile([P, CHUNK], F32, name=f"half{c}_{m}", align_bytes=ALIGN) for m in range(2)]
-                mine = c % 2
-                other = 1 - mine
-                nc.scalar.copy(out=halves[mine][:], in_=sums[mine])
-                nc.vector.tensor_copy(out=halves[other][:], in_=sums[other])
-                nc.scalar.dma_start(out=out[mine * P : (mine + 1) * P, tokens(c)], in_=halves[mine][:])
-                nc.sync.dma_start(out=out[other * P : (other + 1) * P, tokens(c)], in_=halves[other][:])
+            if c == CHUNKS - 1:
+                halves = [keep.tile([P, CHUNK], F32, name=f"last_half{m}", align_bytes=ALIGN) for m in range(2)]
+                nc.scalar.copy(out=halves[1][:], in_=sums[1])
+                nc.vector.tensor_copy(out=halves[0][:], in_=sums[0])
+                nc.scalar.dma_start(out=out[P : 2 * P, tokens(c)], in_=halves[1][:])
+                nc.sync.dma_start(out=out[0:P, tokens(c)], in_=halves[0][:])
                 return
             result = results[:, :, tokens(c)]
-            if c == SCALAR_CHUNK:
+            if c == CHUNKS - 2:
+                nc.scalar.copy(out=result[:, 0], in_=sums[0])
+                nc.vector.tensor_copy(out=result[:, 1], in_=sums[1])
+            elif c == SCALAR_CHUNK:
                 nc.scalar.copy(out=result, in_=sums[:])
             else:
                 nc.vector.tensor_copy(out=result, in_=sums[:])
             if c in STORE_FROM:
                 cols = slice(STORE_FROM[c] * CHUNK, (c + 1) * CHUNK)
-                nc.sync.dma_start(out=out_halves[:, :, cols], in_=results[:, :, cols])
+                queue = nc.scalar if c == SCALAR_CHUNK else nc.sync
+                queue.dma_start(out=out_halves[:, :, cols], in_=results[:, :, cols])
 
         activated = [hidden(c) for c in range(H_AHEAD)]
         summed = []

@@ -20,7 +20,7 @@ ALIGN = 256
 PACK = 4
 LIST_ROWS = 16
 BLOCKS = 16
-STAGED = slice(16, 16 + BLOCKS)
+STAGED = slice(P - BLOCKS, P)
 GATHERS = [128, 128, 256, 256, 256]
 GATHER_AT = [sum(GATHERS[:g]) for g in range(len(GATHERS))]
 CHUNK = 128
@@ -69,8 +69,7 @@ def tile_picked_lora_gelu_p_kernel(tc, x_words, x_scales, w1_words, w1_scales, w
 
         identity = keep.tile([P, P], F32, name="identity", align_bytes=ALIGN)
         make_identity(nc, identity[:])
-        for rows in (slice(0, STAGED.start), slice(STAGED.stop, 64), slice(64, P)):
-            nc.vector.memset(scale_window[rows, :].bitcast(I32), 0)
+        nc.vector.memset(scale_window[0 : STAGED.start, :].bitcast(I32), 0)
         nc.vector.memset(preload[:, 0:1], 0.0)
         nc.vector.memset(early_plane[:].bitcast(I32), 0)
         nc.vector.memset(late_planes[:].bitcast(I32), 0)

@@ -183,8 +183,8 @@ def tile_picked_lora_gelu_p_kernel(tc, x_words, x_scales, w1_words, w1_scales, w
                 return
             result = results[:, :, tokens(c)]
             if c == CHUNKS - 2:
-                nc.scalar.copy(out=result[:, 0], in_=sums[0])
-                nc.vector.tensor_copy(out=result[:, 1], in_=sums[1])
+                nc.vector.tensor_copy(out=result[:, 0], in_=sums[0])
+                nc.scalar.copy(out=result[:, 1], in_=sums[1])
             elif c == SCALAR_CHUNK:
                 nc.scalar.copy(out=result, in_=sums[:])
             else:

from contextlib import ExitStack

import concourse.mybir as mybir
from concourse.masks import make_identity

K, T, S, H, N = 512, 2048, 1024, 512, 256
FLOPS = 2 * S * (K * H + K * N + H * N)

F32 = mybir.dt.float32
BF16 = mybir.dt.bfloat16
I32 = mybir.dt.int32
U32 = mybir.dt.uint32
U16 = mybir.dt.uint16
U8 = mybir.dt.uint8
FP8X4 = mybir.dt.float8_e4m3fn_x4
GELU = mybir.ActivationFunctionType.Gelu_apprx_tanh

P = 128
ALIGN = 256
PACK = 4
LIST_ROWS = 16
BLOCKS = 16
STAGED = slice(P - BLOCKS, P)
GATHERS = [128, 128, 256, 256, 256]
GATHER_AT = [sum(GATHERS[:g]) for g in range(len(GATHERS))]
CHUNK = 128
CHUNKS = S // CHUNK
EARLY = 5 * CHUNK
LATE = S - EARLY
HALF = 64
WARM_UP = [256, 256, 128]
WARM_TRANSPOSES = 5
H_BANKS = [0, 1, 2, 3, 0, 2, 3, 0]
H_AHEAD = 5
OUT_BANKS = [(4,), (5,), (6,), (7,), (1,), (4,), (5, 2), (6, 3)]
SCALAR_CHUNK = 5
STORE_FROM = {1: 0, 2: 2, 3: 3, 4: 4, 5: 5, 6: 6}
DRAIN_LAG = 3
H_CODE_BUFFERS = [0, 1, 2, 0, 1, 2, 0, 1]


def words_of(dram):
    return dram[0].rearrange("p n t -> p (n t)").bitcast(I32)


def tile_picked_lora_gelu_p_kernel(tc, x_words, x_scales, w1_words, w1_scales, w2, w3_words, w3_scales, offs, out):
    nc = tc.nc
    with ExitStack() as ctx:
        keep = ctx.enter_context(tc.tile_pool(name="keep", bufs=1))
        psum = ctx.enter_context(tc.psum_pool(name="psum", bufs=1))

        offsets = keep.tile([P, S // LIST_ROWS], U16, name="offsets", align_bytes=ALIGN)
        scale_window = keep.tile([P, T], U8, name="scale_window", tag="scale_window", align_bytes=ALIGN)
        word_window = keep.tile([P, T], U32, name="word_window", align_bytes=ALIGN)
        w2_raw = keep.tile([P, PACK, H], F32, name="w2_raw", tag="w2_raw", align_bytes=ALIGN)
        w2_bf16 = [[keep.tile([P, 2, HALF, PACK], BF16, name=f"w2_bf16_{a}{u}", align_bytes=ALIGN) for u in range(2)] for a in range(2)]
        w2_words = keep.tile([P, H], U32, name="w2_words", align_bytes=ALIGN)
        w2_plane = keep.tile([P, H], U8, name="w2_plane", align_bytes=ALIGN)
        preload = keep.tile([P, 2], F32, name="preload", align_bytes=ALIGN)
        early_plane = keep.tile([P, EARLY], U8, name="early_plane", align_bytes=ALIGN)
        late_planes = keep.tile([P, LATE + 2 * N], U8, name="late_planes", align_bytes=ALIGN)
        w1_cols = slice(LATE, LATE + N)
        w3_cols = slice(LATE + N, LATE + 2 * N)
        w1_plane = late_planes[:, w1_cols]
        w3_plane = late_planes[:, w3_cols]
        picked_early = keep.tile([P, EARLY], U8, name="picked_early", align_bytes=ALIGN)
        picked_late = keep.tile([P, LATE], U8, name="picked_late", align_bytes=ALIGN)
        x_codes = [keep.tile([P, width], U32, name=f"x_codes{g}", align_bytes=ALIGN) for g, width in enumerate(GATHERS)]

        identity = keep.tile([P, P], F32, name="identity", align_bytes=ALIGN)
        make_identity(nc, identity[:])
        nc.vector.memset(scale_window[0 : STAGED.start, :].bitcast(I32), 0)
        nc.vector.memset(preload[:, 0:1], 0.0)
        nc.vector.memset(early_plane[:].bitcast(I32), 0)
        nc.vector.memset(late_planes[:].bitcast(I32), 0)
        nc.scalar.dma_start(out=scale_window[STAGED, :].bitcast(I32), in_=x_scales[0].bitcast(I32))
        nc.scalar.activation(out=preload[:, 1:2], in_=preload[:, 0:1], func=GELU)

        w2_rows = w2.rearrange("(p j) c -> p j c", j=PACK)
        nc.sync.dma_start(offsets[:], offs)
        nc.sync.dma_start(out=w2_raw[:], in_=w2_rows)
        nc.sync.dma_start(out=word_window[:].bitcast(I32), in_=words_of(x_words))

        def place_scales(plane, rows):
            for r in range(4):
                nc.sync.dma_start(out=plane[r:P:32, :].bitcast(I32), in_=rows[STAGED.start + r : STAGED.stop : 4, :].bitcast(I32))

        nc.vector.tensor_copy(picked_early[:], scale_window[:].indirect(offsets[:, 0 : EARLY // LIST_ROWS]))
        nc.vector.tensor_copy(picked_late[:], scale_window[:].indirect(offsets[:, EARLY // LIST_ROWS : S // LIST_ROWS]))
        place_scales(early_plane, picked_early)
        late_rows = keep.tile([P, LATE + 2 * N], U8, name="late_rows", tag="scale_window", align_bytes=ALIGN)
        nc.sync.dma_start(out=late_rows[STAGED, w1_cols].bitcast(I32), in_=w1_scales[0].bitcast(I32))
        nc.sync.dma_start(out=late_rows[STAGED, w3_cols].bitcast(I32), in_=w3_scales[0].bitcast(I32))

        w2_groups = w2_raw[:].rearrange("p j (m t) -> p m j t", t=PACK)
        for u in range(2):
            for a, copy in enumerate((nc.scalar.copy, nc.vector.tensor_copy)):
                copy(out=w2_bf16[a][u][:].rearrange("p e m j -> p m j e"), in_=w2_groups[:, a * HALF : (a + 1) * HALF, :, 2 * u : 2 * u + 2])
        w_words = keep.tile([P, 2 * N], U32, name="w_words", tag="w2_raw", align_bytes=ALIGN)
        w1_codes = w_words[:, 0:N]
        w3_codes = w_words[:, N : 2 * N]
        nc.sync.dma_start(out=w1_codes.bitcast(I32), in_=words_of(w1_words))
        nc.sync.dma_start(out=w3_codes.bitcast(I32), in_=words_of(w3_words))
        scrap = psum.tile([P, 4 * P], F32, name="scrap", tag="bank7")
        pairs = w2_bf16[0][0][:, 0].rearrange("p m j -> p (m j)").bitcast(F32)
        for n in range(WARM_TRANSPOSES):
            nc.tensor.transpose(scrap[:, (n % PACK) * P : (n % PACK + 1) * P], pairs, identity[:])
        nc.vector.tensor_copy(out=late_rows[:, 0:LATE].bitcast(I32), in_=picked_late[:].bitcast(I32))
        place_scales(late_planes, late_rows)
        for u, a in ((0, 0), (0, 1), (1, 1), (1, 0)):
            for e in range(2):
                first = (2 * u + e) * P + a * HALF
                cols = slice(first, first + HALF)
                nc.vector.quantize_mx(out=w2_words[:, cols].bitcast(FP8X4), scales=w2_plane[:, cols], in_=w2_bf16[a][u][:, e].rearrange("p m j -> p (m j)"))
        for width in WARM_UP:
            nc.tensor.matmul_mx(out=scrap[:, 0:width], lhsT=w2_words[:, 0:P].bitcast(FP8X4), lhsT_scale=w2_plane[:, 0:P], rhs=w2_words[:, 0:width].bitcast(FP8X4), rhs_scale=w2_plane[:, 0:width], start=True, stop=True)
        for g, width in enumerate(GATHERS):
            entries = slice(GATHER_AT[g] // LIST_ROWS, (GATHER_AT[g] + width) // LIST_ROWS)
            nc.vector.tensor_copy(x_codes[g][:], word_window[:].indirect(offsets[:, entries]))

        out_halves = out.rearrange("(m p) n -> p m n", p=P)
        results = keep.tile([P, 2, S - CHUNK], F32, name="results", align_bytes=ALIGN)

        def tokens(c):
            return slice(c * CHUNK, (c + 1) * CHUNK)

        def steps(c):
            width = CHUNK // 2 if c == CHUNKS - 1 else CHUNK
            return [slice(at, at + width) for at in range(0, CHUNK, width)]

        def x_operand(c):
            width = CHUNK
            g = max(n for n, at in enumerate(GATHER_AT) if at <= c * CHUNK)
            word_at = c * CHUNK - GATHER_AT[g]
            byte_at = c * CHUNK
            plane = early_plane[:, byte_at : byte_at + width] if byte_at < EARLY else late_planes[:, byte_at - EARLY : byte_at - EARLY + width]
            return x_codes[g][:, word_at : word_at + width], plane

        def product(dst, codes, plane, block, moving_codes, moving_plane, start, stop):
            cols = slice(block * P, (block + 1) * P)
            nc.tensor.matmul_mx(out=dst, lhsT=codes[:, cols].bitcast(FP8X4), lhsT_scale=plane[:, cols], rhs=moving_codes.bitcast(FP8X4), rhs_scale=moving_plane, start=start, stop=stop)

        def activate(c, sums):
            h_bf16 = keep.tile([P, CHUNK, PACK], BF16, name=f"h_bf16_{c}", align_bytes=ALIGN)
            for part in steps(c):
                nc.scalar.activation(out=h_bf16[:, part], in_=sums[:, :, part].rearrange("p t n -> p n t"), func=GELU)
            return h_bf16

        def hidden(c):
            bank = psum.tile([P, PACK, CHUNK], F32, name="h_sums", tag=f"bank{H_BANKS[c]}")
            for t in range(PACK):
                product(bank[:, t, :], w2_words, w2_plane, t, *x_operand(c), True, True)
            return activate(c, bank[:])

        def open_sums(c):
            banks = OUT_BANKS[c]
            if len(banks) == 2:
                tiles = [psum.tile([P, CHUNK], F32, name=f"out_half{m}", tag=f"bank{banks[m]}")[:] for m in range(2)]
                halves = tiles
            else:
                tiles = psum.tile([P, 2, CHUNK], F32, name="out_both", tag=f"bank{banks[0]}")
                halves = [tiles[:, m, :] for m in range(2)]
            for m in range(2):
                product(halves[m], w1_codes, w1_plane, m, *x_operand(c), c >= CHUNKS - 2 or m == 0, False)
            return tiles, halves

        def close_sums(c, h_bf16, halves):
            h_words = keep.tile([P, CHUNK], U32, name="h_words", tag=f"h_words{H_CODE_BUFFERS[c]}", align_bytes=ALIGN)
            h_plane = keep.tile([P, CHUNK], U8, name="h_plane", tag=f"h_plane{H_CODE_BUFFERS[c]}", align_bytes=ALIGN)
            h_operand = (h_words[:], h_plane[:])
            for part in steps(c):
                nc.vector.quantize_mx(out=h_words[:, part].bitcast(FP8X4), scales=h_plane[:, part], in_=h_bf16[:, part].rearrange("p n t -> p (n t)"))
            for m in range(2):
                product(halves[m], w3_codes, w3_plane, m, *h_operand, False, c >= CHUNKS - 2 or m == 1)

        def drain(c, sums):
            if c == CHUNKS - 1:
                halves = [keep.tile([P, CHUNK], F32, name=f"last_half{m}", align_bytes=ALIGN) for m in range(2)]
                nc.scalar.copy(out=halves[1][:], in_=sums[1])
                nc.vector.tensor_copy(out=halves[0][:], in_=sums[0])
                nc.scalar.dma_start(out=out[P : 2 * P, tokens(c)], in_=halves[1][:])
                nc.sync.dma_start(out=out[0:P, tokens(c)], in_=halves[0][:])
                return
            result = results[:, :, tokens(c)]
            if c == CHUNKS - 2:
                nc.vector.tensor_copy(out=result[:, 0], in_=sums[0])
                nc.scalar.copy(out=result[:, 1], in_=sums[1])
            elif c == SCALAR_CHUNK:
                nc.scalar.copy(out=result, in_=sums[:])
            else:
                nc.vector.tensor_copy(out=result, in_=sums[:])
            if c in STORE_FROM:
                cols = slice(STORE_FROM[c] * CHUNK, (c + 1) * CHUNK)
                queue = nc.scalar if c == SCALAR_CHUNK else nc.sync
                queue.dma_start(out=out_halves[:, :, cols], in_=results[:, :, cols])

        activated = [hidden(c) for c in range(H_AHEAD)]
        summed = []
        for c in range(CHUNKS + DRAIN_LAG):
            if c >= DRAIN_LAG:
                drain(c - DRAIN_LAG, summed[c - DRAIN_LAG])
            if c < CHUNKS:
                tiles, halves = open_sums(c)
                close_sums(c, activated[c], halves)
                summed.append(tiles)
            if c >= 1 and len(activated) < CHUNKS:
                activated.append(hidden(len(activated)))
